import numpy as np
import ml_dtypes


def mxq(x, axis, fmt="e4m3"):
    dtype, down = {"e4m3": (ml_dtypes.float8_e4m3fn, 7), "e5m2": (ml_dtypes.float8_e5m2, 14)}[fmt]
    v = np.moveaxis(np.asarray(x, np.float32).astype(ml_dtypes.bfloat16).astype(np.float64), axis, -1)
    blocks = v.reshape(v.shape[:-1] + (-1, 32))
    amax = np.abs(blocks).max(-1, keepdims=True)
    byte = np.maximum(np.where(amax > 0, np.frexp(amax)[1] - 1 + 127, 0) - down, 1)
    scale = np.exp2(byte - 127.0)
    codes = (blocks / scale).astype(np.float32).astype(dtype).astype(np.float64)
    return np.moveaxis((codes * scale).reshape(v.shape), -1, axis)


WIDE = False


def mx_kscale(k):
    if not WIDE:
        return np.ones(k)
    levels = np.array([24, -24, 12, -12, 0])
    if k % 512:
        return np.exp2(np.random.permutation(np.resize(levels, k // 32))).repeat(32)
    a = np.empty((k // 512, 16))
    for p in range(k // 512):
        a[p, :8] = np.random.permutation(np.resize(levels, 8))
        for g in range(8):
            far = levels[np.abs(levels - a[p, g]) >= 10]
            a[p, g + 8] = far[np.random.randint(len(far))]
    return np.exp2(a.ravel()).repeat(32)


def f64(x):
    return np.asarray(x).astype(np.float64)


def striped(idx):
    return np.tile(idx.reshape(-1, 16).T, (8, 1)).astype(np.uint16)


def unstriped(offs):
    return offs[:16].T.reshape(-1).astype(np.int64)


E2M1 = np.array([0.0, 0.5, 1.0, 1.5, 2.0, 3.0, 4.0, 6.0, -0.0, -0.5, -1.0, -1.5, -2.0, -3.0, -4.0, -6.0])


def pack_weight(w, fmt):
    k, n = w.shape
    w = f64(np.asarray(w, np.float32).astype(ml_dtypes.bfloat16)).reshape(k // 32, 32, n)
    amax = np.abs(w).max(1)
    if fmt == "e4m3":
        byte = np.frexp(amax)[1] - 1 + 127 - 7
    else:
        mant, ex = np.frexp(amax / 6.0)
        byte = np.where(mant > 0.5, ex, ex - 1) + 127
    byte = np.clip(np.where(amax > 0, byte, 1), 1, 254)
    scaled = (w * np.exp2(127.0 - byte)[:, None, :]).reshape(k, n).astype(np.float32)
    by_word = np.ascontiguousarray(scaled.reshape(k // 512, 128, 4, n).transpose(0, 1, 3, 2))
    if fmt == "e4m3":
        words = by_word.astype(ml_dtypes.float8_e4m3fn).view(np.uint8)
    else:
        c = by_word.astype(ml_dtypes.float4_e2m1fn).view(np.uint8) & 0xF
        words = (c[..., 0::2] | (c[..., 1::2] << 4)).reshape(k // 512, 128, 2 * n)
    return np.ascontiguousarray(words), np.ascontiguousarray(byte.astype(np.uint8).reshape(k // 512, 16, n))


def unpack_weight(words, scales, fmt):
    g, _, n = scales.shape
    words = np.ascontiguousarray(words).reshape(g, 128, n, -1)
    if fmt == "e4m3":
        vals = words.view(ml_dtypes.float8_e4m3fn).astype(np.float64)
    else:
        nib = np.empty((g, 128, n, 4), np.uint8)
        nib[..., 0::2] = words & 0xF
        nib[..., 1::2] = words >> 4
        vals = E2M1[nib]
    vals = vals * np.repeat(np.exp2(scales.astype(np.float64) - 127.0), 8, axis=1)[..., None]
    return vals.transpose(0, 1, 3, 2).reshape(g * 512, n)


def pack_table4(v):
    words, scales = pack_weight(v, "e2m1")
    g, t = words.shape[0] // 2, v.shape[1]
    return np.ascontiguousarray(words.reshape(g, 2, 128, t, 2).transpose(0, 2, 3, 1, 4).reshape(g, 128, t, 4)), scales


def unpack_table4(words, scales):
    g, _, t, _ = words.shape
    return unpack_weight(words.reshape(g, 128, t, 2, 2).transpose(0, 3, 1, 2, 4).reshape(2 * g, 128, 2 * t), scales, "e2m1")


K, R, M, T, N, J = 1024, 1024, 1024, 4096, 512, 1024


def setup_inputs():
    n = np.random.standard_normal
    u = mx_kscale(R)[:, None]
    s = mx_kscale(K)[:, None]
    p_tab = pack_table4(n((R, T)) * u)
    return {
        "x": (n((K, M)) * s).astype(np.float32),
        "w": (n((K, R)) / np.sqrt(K) / s / u.T).astype(np.float32),
        "tab_words": p_tab[0],
        "tab_scales": p_tab[1],
        "wv": (n((R, N)) / np.sqrt(R) / u).astype(np.float32),
        "offs": striped(np.random.permutation(T)[:J]),
    }


def reference(x, w, tab_words, tab_scales, wv, offs):
    idx = unstriped(offs)
    x_ = mxq(f64(x), 0, "e4m3")
    w_ = mxq(f64(w), 0, "e4m3")
    qa = w_.T @ x_
    qa_ = mxq(qa, 0, "e4m3")
    tab_ = unpack_table4(tab_words, tab_scales)[:, idx]
    sc = qa_.T @ tab_
    wv_ = mxq(f64(wv), 0, "e4m3")
    vv = wv_.T @ tab_
    return sc * 0.03125, vv

@@ -1,0 +1,188 @@
+from contextlib import ExitStack
+
+import concourse.mybir as mybir
+
+K, R, M, T, N, J = 1024, 1024, 1024, 4096, 512, 1024
+FLOPS = 2 * (K * R * M + R * M * J + R * N * J)
+
+F32 = mybir.dt.float32
+BF16 = mybir.dt.bfloat16
+I32 = mybir.dt.int32
+U32 = mybir.dt.uint32
+U16 = mybir.dt.uint16
+U8 = mybir.dt.uint8
+FP8X4 = mybir.dt.float8_e4m3fn_x4
+FP4X4 = mybir.dt.float4_e2m1fn_x4
+COPY = mybir.ActivationFunctionType.Copy
+
+P = 128
+PACK = 4
+KP = P * PACK
+W = 512
+HALF = W // 2
+SCORE_SCALE = 0.03125
+
+
+def tile_list_mlat_scale_kernel(tc, x, w, tab_words, tab_scales, wv, offs, out_0, out_1):
+    nc = tc.nc
+    with ExitStack() as ctx:
+        keep = ctx.enter_context(tc.tile_pool(name="keep", bufs=1))
+        stage = ctx.enter_context(tc.tile_pool(name="stage", bufs=4))
+        psum = ctx.enter_context(tc.psum_pool(name="psum", bufs=8))
+
+        offsets = keep.tile([P, J // 16], U16, name="offsets")
+        scale_rows = keep.tile([P, T // 4], I32, name="scale_rows", align_bytes=64)
+        picked_scales = keep.tile([P, J], U8, name="picked_scales", align_bytes=64)
+        tab_planes = keep.tile([P, 2 * J // 4], I32, name="tab_planes", align_bytes=64)
+        table = keep.tile([P, T], I32, name="table", align_bytes=64)
+
+        nc.vector.memset(scale_rows[:], 0)
+        nc.vector.memset(tab_planes[:], 0)
+
+        def load(name, src):
+            raw = keep.tile([P, PACK, W], F32, name=name, align_bytes=64)
+            nc.sync.dma_start(out=raw[:], in_=src.rearrange("(p j) c -> p j c", j=PACK))
+            return raw
+
+        def rows(a):
+            return slice(a * KP, (a + 1) * KP)
+
+        def cols(h):
+            return slice(h * W, (h + 1) * W)
+
+        raw = {}
+        raw["w", 0, 0] = load("w00", w[rows(0), cols(0)])
+        nc.sync.dma_start(offsets[:], offs)
+        nc.sync.dma_start(out=scale_rows[0:P:4, :], in_=tab_scales.bitcast(I32).rearrange("a q n -> q a n"))
+        raw["x", 0, 0] = load("x00", x[rows(0), cols(0)])
+        raw["w", 0, 1] = load("w01", w[rows(1), cols(0)])
+        raw["x", 0, 1] = load("x01", x[rows(1), cols(0)])
+        raw["w", 1, 0] = load("w10", w[rows(0), cols(1)])
+        raw["w", 1, 1] = load("w11", w[rows(1), cols(1)])
+        raw["x", 1, 0] = load("x10", x[rows(0), cols(1)])
+        raw["x", 1, 1] = load("x11", x[rows(1), cols(1)])
+        nc.sync.dma_start(out=table[:], in_=tab_words[0].rearrange("p t b -> p (t b)").bitcast(I32))
+        raw["v", 0, 0] = load("v00", wv[rows(0), :])
+        raw["v", 0, 1] = load("v01", wv[rows(1), :])
+
+        codes = {}
+        scales = {}
+
+        def quantise(key):
+            src = raw[key]
+            name = "%s%d%d" % key
+            grouped = stage.tile([P, W * PACK], BF16, name="grouped", align_bytes=64)
+            for half, copy in enumerate((nc.vector.tensor_copy, nc.scalar.copy)):
+                dst = grouped[:, half * HALF * PACK : (half + 1) * HALF * PACK]
+                if key[0] == "w":
+                    copy(
+                        out=dst.rearrange("p (t m j) -> p m j t", t=2, j=PACK),
+                        in_=src[:].rearrange("p j (m t) -> p m j t", t=PACK)[:, :, :, 2 * half : 2 * half + 2],
+                    )
+                else:
+                    copy(
+                        out=dst.rearrange("p (c i j) -> p c j i", i=4, j=PACK),
+                        in_=src[:, :, half * HALF : (half + 1) * HALF].rearrange("p j (c i) -> p c j i", i=4),
+                    )
+            codes[key] = keep.tile([P, W], U32, name="codes_" + name, align_bytes=64)
+            scales[key] = keep.tile([P, W], U8, name="scales_" + name, align_bytes=64)
+            for half in range(2):
+                part = slice(half * HALF, (half + 1) * HALF)
+                nc.vector.quantize_mx(
+                    out=codes[key][:, part].bitcast(FP8X4),
+                    scales=scales[key][:, part],
+                    in_=grouped[:, half * HALF * PACK : (half + 1) * HALF * PACK],
+                )
+
+        def project(b, pair):
+            h = pair // 2
+            qa_bf = stage.tile([P, 2 * W], BF16, name="qa_bf", align_bytes=64)
+            for u in range(2):
+                m0 = (pair % 2) * 2 * P + u * P
+                bank = psum.tile([P, W], F32, name="bank")
+                for t in range(PACK):
+                    for a in range(2):
+                        nc.tensor.matmul_mx(
+                            out=bank[:, t * P : (t + 1) * P],
+                            lhsT=codes["w", b, a][:, t * P : (t + 1) * P].bitcast(FP8X4),
+                            lhsT_scale=scales["w", b, a][:, t * P : (t + 1) * P],
+                            rhs=codes["x", h, a][:, m0 : m0 + P].bitcast(FP8X4),
+                            rhs_scale=scales["x", h, a][:, m0 : m0 + P],
+                            start=(a == 0),
+                            stop=(a == 1),
+                        )
+                nc.scalar.copy(
+                    out=qa_bf[:, u * W : (u + 1) * W].rearrange("p (m t) -> p m t", t=PACK),
+                    in_=bank[:].rearrange("p (t m) -> p m t", t=PACK),
+                )
+            key = ("q", pair, b)
+            codes[key] = keep.tile([P, 2 * P], U32, name="codes_q%d%d" % (pair, b), align_bytes=64)
+            scales[key] = keep.tile([P, 2 * P], U8, name="scales_q%d%d" % (pair, b), align_bytes=64)
+            nc.vector.quantize_mx(out=codes[key][:].bitcast(FP8X4), scales=scales[key][:], in_=qa_bf[:])
+
+        def pick_scales():
+            nc.vector.tensor_copy(picked_scales[:], scale_rows[:].bitcast(U8).indirect(offsets[:]))
+            for quad in range(4):
+                nc.gpsimd.dma_start(
+                    out=tab_planes[32 * quad : 32 * quad + 4, :],
+                    in_=picked_scales[32 * quad : 32 * quad + 32 : 4, :].bitcast(I32),
+                )
+
+        parted = {}
+
+        def pick_words(jh):
+            picked = keep.tile([P, W], U32, name="picked%d" % jh, align_bytes=64)
+            nc.vector.tensor_copy(picked[:], table[:].bitcast(U32).indirect(offsets[:, jh * W // 16 : (jh + 1) * W // 16]))
+            parted[jh] = keep.tile([P, 2, 2 * W], U8, name="parted%d" % jh, align_bytes=64)
+            nc.vector.tensor_copy(
+                out=parted[jh][:].bitcast(U16),
+                in_=picked[:].bitcast(U16).rearrange("p (j d) -> p d j", d=2),
+            )
+
+        def against_table(name, keys, c0, dest, factor):
+            result = keep.tile([P, J], F32, name=name, align_bytes=64)
+            for jh in range(2):
+                bank = psum.tile([P, W], F32, name="bank")
+                for b in range(2):
+                    nc.tensor.matmul_mx(
+                        out=bank[:],
+                        lhsT=codes[keys[b]][:, c0 : c0 + P].bitcast(FP8X4),
+                        lhsT_scale=scales[keys[b]][:, c0 : c0 + P],
+                        rhs=parted[jh][:, b, :].bitcast(FP4X4),
+                        rhs_scale=tab_planes[:].bitcast(U8)[:, b * J + jh * W : b * J + (jh + 1) * W],
+                        start=(b == 0),
+                        stop=(b == 1),
+                    )
+                if jh == 0:
+                    nc.scalar.activation(out=result[:, cols(jh)], in_=bank[:], func=COPY, scale=factor)
+                else:
+                    nc.vector.tensor_scalar_mul(out=result[:, cols(jh)], in0=bank[:], scalar1=factor)
+            nc.sync.dma_start(out=dest, in_=result[:])
+
+        quantise(("w", 0, 0))
+        quantise(("x", 0, 0))
+        pick_scales()
+        quantise(("w", 0, 1))
+        quantise(("x", 0, 1))
+        project(0, 0)
+        quantise(("w", 1, 0))
+        project(0, 1)
+        quantise(("w", 1, 1))
+        project(1, 0)
+        quantise(("x", 1, 0))
+        project(1, 1)
+        quantise(("x", 1, 1))
+        project(0, 2)
+        project(1, 2)
+        pick_words(0)
+        pick_words(1)
+        project(0, 3)
+        project(1, 3)
+        quantise(("v", 0, 0))
+        quantise(("v", 0, 1))
+        for mt in range(M // P):
+            keys = [("q", mt // 2, b) for b in range(2)]
+            against_table("scores%d" % mt, keys, (mt % 2) * P, out_0[mt * P : (mt + 1) * P, :], SCORE_SCALE)
+        for nt in range(N // P):
+            keys = [("v", 0, a) for a in range(2)]
+            against_table("values%d" % nt, keys, nt * P, out_1[nt * P : (nt + 1) * P, :], 1.0)

@@ -26,23 +26,12 @@ SCORE_SCALE = 0.03125
 def tile_list_mlat_scale_kernel(tc, x, w, tab_words, tab_scales, wv, offs, out_0, out_1):
     nc = tc.nc
     with ExitStack() as ctx:
+        lists = ctx.enter_context(tc.tile_pool(name="lists", bufs=1))
         keep = ctx.enter_context(tc.tile_pool(name="keep", bufs=1))
-        stage = ctx.enter_context(tc.tile_pool(name="stage", bufs=4))
         psum = ctx.enter_context(tc.psum_pool(name="psum", bufs=8))
 
-        offsets = keep.tile([P, J // 16], U16, name="offsets")
-        scale_rows = keep.tile([P, T // 4], I32, name="scale_rows", align_bytes=64)
-        picked_scales = keep.tile([P, J], U8, name="picked_scales", align_bytes=64)
-        tab_planes = keep.tile([P, 2 * J // 4], I32, name="tab_planes", align_bytes=64)
-        table = keep.tile([P, T], I32, name="table", align_bytes=64)
-
-        nc.vector.memset(scale_rows[:], 0)
-        nc.vector.memset(tab_planes[:], 0)
-
-        def load(name, src):
-            raw = keep.tile([P, PACK, W], F32, name=name, align_bytes=64)
-            nc.sync.dma_start(out=raw[:], in_=src.rearrange("(p j) c -> p j c", j=PACK))
-            return raw
+        def tile(name, shape, dtype, slot=None):
+            return keep.tile(shape, dtype, name=name, tag=slot or name, align_bytes=64)
 
         def rows(a):
             return slice(a * KP, (a + 1) * KP)
@@ -50,53 +39,46 @@ def tile_list_mlat_scale_kernel(tc, x, w, tab_words, tab_scales, wv, offs, out_0
         def cols(h):
             return slice(h * W, (h + 1) * W)
 
-        raw = {}
-        raw["w", 0, 0] = load("w00", w[rows(0), cols(0)])
-        nc.sync.dma_start(offsets[:], offs)
-        nc.sync.dma_start(out=scale_rows[0:P:4, :], in_=tab_scales.bitcast(I32).rearrange("a q n -> q a n"))
-        raw["x", 0, 0] = load("x00", x[rows(0), cols(0)])
-        raw["w", 0, 1] = load("w01", w[rows(1), cols(0)])
-        raw["x", 0, 1] = load("x01", x[rows(1), cols(0)])
-        raw["w", 1, 0] = load("w10", w[rows(0), cols(1)])
-        raw["w", 1, 1] = load("w11", w[rows(1), cols(1)])
-        raw["x", 1, 0] = load("x10", x[rows(0), cols(1)])
-        raw["x", 1, 1] = load("x11", x[rows(1), cols(1)])
-        nc.sync.dma_start(out=table[:], in_=tab_words[0].rearrange("p t b -> p (t b)").bitcast(I32))
-        raw["v", 0, 0] = load("v00", wv[rows(0), :])
-        raw["v", 0, 1] = load("v01", wv[rows(1), :])
+        def load(name, src, slot=None):
+            raw = tile(name, [P, PACK, src.shape[1]], F32, slot)
+            nc.sync.dma_start(out=raw[:], in_=src.rearrange("(p j) c -> p j c", j=PACK))
+            return raw
 
         codes = {}
         scales = {}
 
-        def quantise(key):
-            src = raw[key]
+        def quantise(key, src, shares):
             name = "%s%d%d" % key
-            grouped = stage.tile([P, W * PACK], BF16, name="grouped", align_bytes=64)
-            for half, copy in enumerate((nc.vector.tensor_copy, nc.scalar.copy)):
-                dst = grouped[:, half * HALF * PACK : (half + 1) * HALF * PACK]
+            codes[key] = tile("codes_" + name, [P, W], U32)
+            scales[key] = tile("scales_" + name, [P, W], U8)
+            width = W // len(shares)
+            grouped = []
+            for s, (copy, slot) in enumerate(shares):
+                dst = tile("grouped_%s_%d" % (name, s), [P, width * PACK], BF16, slot)
                 if key[0] == "w":
                     copy(
-                        out=dst.rearrange("p (t m j) -> p m j t", t=2, j=PACK),
-                        in_=src[:].rearrange("p j (m t) -> p m j t", t=PACK)[:, :, :, 2 * half : 2 * half + 2],
+                        out=dst[:].rearrange("p (t m j) -> p m j t", t=2, j=PACK),
+                        in_=src.rearrange("p j (m t) -> p m j t", t=PACK)[:, :, :, 2 * s : 2 * s + 2],
                     )
                 else:
                     copy(
-                        out=dst.rearrange("p (c i j) -> p c j i", i=4, j=PACK),
-                        in_=src[:, :, half * HALF : (half + 1) * HALF].rearrange("p j (c i) -> p c j i", i=4),
+                        out=dst[:].rearrange("p (c i j) -> p c j i", i=4, j=PACK),
+                        in_=src[:, :, s * width : (s + 1) * width].rearrange("p j (c i) -> p c j i", i=4),
                     )
-            codes[key] = keep.tile([P, W], U32, name="codes_" + name, align_bytes=64)
-            scales[key] = keep.tile([P, W], U8, name="scales_" + name, align_bytes=64)
-            for half in range(2):
-                part = slice(half * HALF, (half + 1) * HALF)
-                nc.vector.quantize_mx(
-                    out=codes[key][:, part].bitcast(FP8X4),
-                    scales=scales[key][:, part],
-                    in_=grouped[:, half * HALF * PACK : (half + 1) * HALF * PACK],
-                )
+                grouped.append(dst)
+            for s, dst in enumerate(grouped):
+                part = slice(s * width, (s + 1) * width)
+                nc.vector.quantize_mx(out=codes[key][:, part].bitcast(FP8X4), scales=scales[key][:, part], in_=dst[:])
 
-        def project(b, pair):
+        def both(vector_slot=None, scalar_slot=None):
+            return [(nc.vector.tensor_copy, vector_slot), (nc.scalar.copy, scalar_slot)]
+
+        def vector_alone():
+            return [(nc.vector.tensor_copy, None), (nc.vector.tensor_copy, None)]
+
+        def project(pair, b, slot=None):
             h = pair // 2
-            qa_bf = stage.tile([P, 2 * W], BF16, name="qa_bf", align_bytes=64)
+            qa_bf = tile("qa_bf%d%d" % (pair, b), [P, 2 * W], BF16, slot)
             for u in range(2):
                 m0 = (pair % 2) * 2 * P + u * P
                 bank = psum.tile([P, W], F32, name="bank")
@@ -115,74 +97,117 @@ def tile_list_mlat_scale_kernel(tc, x, w, tab_words, tab_scales, wv, offs, out_0
                     out=qa_bf[:, u * W : (u + 1) * W].rearrange("p (m t) -> p m t", t=PACK),
                     in_=bank[:].rearrange("p (t m) -> p m t", t=PACK),
                 )
-            key = ("q", pair, b)
-            codes[key] = keep.tile([P, 2 * P], U32, name="codes_q%d%d" % (pair, b), align_bytes=64)
-            scales[key] = keep.tile([P, 2 * P], U8, name="scales_q%d%d" % (pair, b), align_bytes=64)
-            nc.vector.quantize_mx(out=codes[key][:].bitcast(FP8X4), scales=scales[key][:], in_=qa_bf[:])
-
-        def pick_scales():
-            nc.vector.tensor_copy(picked_scales[:], scale_rows[:].bitcast(U8).indirect(offsets[:]))
-            for quad in range(4):
-                nc.gpsimd.dma_start(
-                    out=tab_planes[32 * quad : 32 * quad + 4, :],
-                    in_=picked_scales[32 * quad : 32 * quad + 32 : 4, :].bitcast(I32),
-                )
+            part = slice((pair % 2) * 2 * P, (pair % 2 + 1) * 2 * P)
+            nc.vector.quantize_mx(
+                out=codes["q", h, b][:, part].bitcast(FP8X4), scales=scales["q", h, b][:, part], in_=qa_bf[:]
+            )
 
         parted = {}
 
-        def pick_words(jh):
-            picked = keep.tile([P, W], U32, name="picked%d" % jh, align_bytes=64)
+        def pick_words(jh, slot):
+            picked = tile("picked%d" % jh, [P, W], U32, slot)
             nc.vector.tensor_copy(picked[:], table[:].bitcast(U32).indirect(offsets[:, jh * W // 16 : (jh + 1) * W // 16]))
-            parted[jh] = keep.tile([P, 2, 2 * W], U8, name="parted%d" % jh, align_bytes=64)
+            parted[jh] = tile("parted%d" % jh, [P, 2, 2 * W], U8)
             nc.vector.tensor_copy(
                 out=parted[jh][:].bitcast(U16),
                 in_=picked[:].bitcast(U16).rearrange("p (j d) -> p d j", d=2),
             )
 
-        def against_table(name, keys, c0, dest, factor):
-            result = keep.tile([P, J], F32, name=name, align_bytes=64)
-            for jh in range(2):
-                bank = psum.tile([P, W], F32, name="bank")
-                for b in range(2):
-                    nc.tensor.matmul_mx(
-                        out=bank[:],
-                        lhsT=codes[keys[b]][:, c0 : c0 + P].bitcast(FP8X4),
-                        lhsT_scale=scales[keys[b]][:, c0 : c0 + P],
-                        rhs=parted[jh][:, b, :].bitcast(FP4X4),
-                        rhs_scale=tab_planes[:].bitcast(U8)[:, b * J + jh * W : b * J + (jh + 1) * W],
-                        start=(b == 0),
-                        stop=(b == 1),
-                    )
-                if jh == 0:
-                    nc.scalar.activation(out=result[:, cols(jh)], in_=bank[:], func=COPY, scale=factor)
-                else:
-                    nc.vector.tensor_scalar_mul(out=result[:, cols(jh)], in0=bank[:], scalar1=factor)
-            nc.sync.dma_start(out=dest, in_=result[:])
+        def against_table(keys, c0, jh, result, factor, on_scalar):
+            bank = psum.tile([P, W], F32, name="bank")
+            for b in range(2):
+                nc.tensor.matmul_mx(
+                    out=bank[:],
+                    lhsT=codes[keys[b]][:, c0 : c0 + P].bitcast(FP8X4),
+                    lhsT_scale=scales[keys[b]][:, c0 : c0 + P],
+                    rhs=parted[jh][:, b, :].bitcast(FP4X4),
+                    rhs_scale=tab_planes[:].bitcast(U8)[:, b * J + jh * W : b * J + (jh + 1) * W],
+                    start=(b == 0),
+                    stop=(b == 1),
+                )
+            if on_scalar:
+                nc.scalar.activation(out=result[:, cols(jh)], in_=bank[:], func=COPY, scale=factor)
+            else:
+                nc.vector.tensor_scalar_mul(out=result[:, cols(jh)], in0=bank[:], scalar1=factor)
 
-        quantise(("w", 0, 0))
-        quantise(("x", 0, 0))
-        pick_scales()
-        quantise(("w", 0, 1))
-        quantise(("x", 0, 1))
+        def score(mt, jh, staged, on_scalar):
+            keys = [("q", mt // 4, b) for b in range(2)]
+            against_table(keys, (mt % 4) * P, jh, staged[:, mt % 4, :], SCORE_SCALE, on_scalar)
+
+        offsets = lists.tile([P, J // 16], U16, name="offsets")
+        scale_rows = tile("scale_rows", [P, T // 4], I32, "raw_x10")
+        picked_scales = tile("picked_scales", [P, J], U8)
+        tab_planes = tile("tab_planes", [P, 2 * J // 4], I32)
+
+        nc.sync.dma_start(out=scale_rows[0:32, :], in_=tab_scales.bitcast(I32).rearrange("a q n -> q a n"))
+        nc.sync.dma_start(offsets[:], offs)
+        nc.vector.memset(scale_rows[32:64, :], 0)
+        nc.vector.memset(scale_rows[64:P, :], 0)
+        nc.vector.memset(tab_planes[:], 0)
+        raw_w = [load("raw_w%d" % a, w[rows(a), :]) for a in range(2)]
+        raw_x0 = [load("raw_x0%d" % a, x[rows(a), cols(0)]) for a in range(2)]
+
+        nc.vector.tensor_copy(picked_scales[:], scale_rows[:].bitcast(U8).indirect(offsets[:]))
+        for quad in range(4):
+            nc.sync.dma_start(
+                out=tab_planes[32 * quad : 32 * quad + 4, :],
+                in_=picked_scales[8 * quad : 8 * quad + 8, :].bitcast(I32),
+            )
+        raw_x1 = [load("raw_x10", x[rows(0), cols(1)])]
+
+        quantise(("w", 0, 0), raw_w[0][:, :, cols(0)], both("raw_x11", "table"))
+        raw_x1.append(load("raw_x11", x[rows(1), cols(1)]))
+        table = tile("table", [P, T], I32)
+        nc.sync.dma_start(out=table[:], in_=tab_words[0].rearrange("p t b -> p (t b)").bitcast(I32))
+        quantise(("w", 1, 0), raw_w[0][:, :, cols(1)], both("raw_v0", "raw_v1"))
+        raw_v = [load("raw_v%d" % a, wv[rows(a), :]) for a in range(2)]
+        quantise(("w", 0, 1), raw_w[1][:, :, cols(0)], both())
+        quantise(("w", 1, 1), raw_w[1][:, :, cols(1)], both())
+        quantise(("x", 0, 0), raw_x0[0][:], both())
+        quantise(("x", 0, 1), raw_x0[1][:], both())
+        quantise(("x", 1, 0), raw_x1[0][:], vector_alone())
+        quantise(("x", 1, 1), raw_x1[1][:], vector_alone())
+
+        def qa_operand(h, b, slot):
+            codes["q", h, b] = tile("codes_q%d%d" % (h, b), [P, W], U32, slot)
+            scales["q", h, b] = tile("scales_q%d%d" % (h, b), [P, W], U8)
+
+        qa_operand(0, 0, "grouped_x11_0")
+        qa_operand(0, 1, "grouped_x11_1")
         project(0, 0)
-        quantise(("w", 1, 0))
         project(0, 1)
-        quantise(("w", 1, 1))
         project(1, 0)
-        quantise(("x", 1, 0))
-        project(1, 1)
-        quantise(("x", 1, 1))
-        project(0, 2)
-        project(1, 2)
-        pick_words(0)
-        pick_words(1)
-        project(0, 3)
-        project(1, 3)
-        quantise(("v", 0, 0))
-        quantise(("v", 0, 1))
-        for mt in range(M // P):
-            keys = [("q", mt // 2, b) for b in range(2)]
-            against_table("scores%d" % mt, keys, (mt % 2) * P, out_0[mt * P : (mt + 1) * P, :], SCORE_SCALE)
+        project(1, 1, "pick_slot")
+        pick_words(0, "pick_slot")
+        pick_words(1, "pick_slot")
+        qa_operand(1, 0, "pick_slot")
+        qa_operand(1, 1, "table")
+        project(2, 0)
+        project(2, 1)
+        project(3, 0)
+        project(3, 1)
+
+        staged = tile("scores0", [P, 4, J], F32, "raw_w0")
+        for jh in range(2):
+            for mt in range(4):
+                score(mt, jh, staged, True)
+                if mt % 2 == 1:
+                    nc.sync.dma_start(
+                        out=out_0[(mt - 1) * P : (mt + 1) * P, cols(jh)].rearrange("(u p) c -> p u c", p=P),
+                        in_=staged[:, mt - 1 : mt + 1, cols(jh)],
+                    )
+        quantise(("v", 0, 0), raw_v[0][:], [(nc.vector.tensor_copy, "qa_bf31")])
+        quantise(("v", 0, 1), raw_v[1][:], [(nc.vector.tensor_copy, "qa_bf31")])
+
+        staged = tile("scores1", [P, 4, J], F32, "raw_w1")
+        for mt in range(4, 8):
+            score(mt, 0, staged, True)
+            score(mt, 1, staged, mt == 4)
+            nc.sync.dma_start(out=out_0[mt * P : (mt + 1) * P, :], in_=staged[:, mt % 4, :])
+
+        values = tile("values", [P, 4, J], F32, "table")
+        keys = [("v", 0, a) for a in range(2)]
         for nt in range(N // P):
-            keys = [("v", 0, a) for a in range(2)]
-            against_table("values%d" % nt, keys, nt * P, out_1[nt * P : (nt + 1) * P, :], 1.0)
+            for jh in range(2):
+                against_table(keys, nt * P, jh, values[:, nt, :], 1.0, jh == 0)
+            nc.sync.dma_start(out=out_1[nt * P : (nt + 1) * P, :], in_=values[:, nt, :])

@@ -52,8 +52,9 @@ def tile_list_mlat_scale_kernel(tc, x, w, tab_words, tab_scales, wv, offs, out_0
             codes[key] = tile("codes_" + name, [P, W], U32)
             scales[key] = tile("scales_" + name, [P, W], U8)
             width = W // len(shares)
-            grouped = []
-            for s, (copy, slot) in enumerate(shares):
+
+            def cast(s):
+                copy, slot = shares[s]
                 dst = tile("grouped_%s_%d" % (name, s), [P, width * PACK], BF16, slot)
                 if key[0] == "w":
                     copy(
@@ -65,8 +66,10 @@ def tile_list_mlat_scale_kernel(tc, x, w, tab_words, tab_scales, wv, offs, out_0
                         out=dst[:].rearrange("p (c i j) -> p c j i", i=4, j=PACK),
                         in_=src[:, :, s * width : (s + 1) * width].rearrange("p j (c i) -> p c j i", i=4),
                     )
-                grouped.append(dst)
-            for s, dst in enumerate(grouped):
+                return dst
+
+            for s in range(len(shares)):
+                dst = cast(s)
                 part = slice(s * width, (s + 1) * width)
                 nc.vector.quantize_mx(out=codes[key][:, part].bitcast(FP8X4), scales=scales[key][:, part], in_=dst[:])
 
@@ -135,7 +138,7 @@ def tile_list_mlat_scale_kernel(tc, x, w, tab_words, tab_scales, wv, offs, out_0
             against_table(keys, (mt % 4) * P, jh, staged[:, mt % 4, :], SCORE_SCALE, on_scalar)
 
         offsets = lists.tile([P, J // 16], U16, name="offsets")
-        scale_rows = tile("scale_rows", [P, T // 4], I32, "raw_x10")
+        scale_rows = tile("scale_rows", [P, T // 4], I32, "raw_v0")
         picked_scales = tile("picked_scales", [P, J], U8)
         tab_planes = tile("tab_planes", [P, 2 * J // 4], I32)
 
@@ -147,20 +150,20 @@ def tile_list_mlat_scale_kernel(tc, x, w, tab_words, tab_scales, wv, offs, out_0
         raw_w = [load("raw_w%d" % a, w[rows(a), :]) for a in range(2)]
         raw_x0 = [load("raw_x0%d" % a, x[rows(a), cols(0)]) for a in range(2)]
 
+        raw_x1 = [load("raw_x1%d" % a, x[rows(a), cols(1)]) for a in range(2)]
+        table = tile("table", [P, T], I32)
+        nc.sync.dma_start(out=table[:], in_=tab_words[0].rearrange("p t b -> p (t b)").bitcast(I32))
+
         nc.vector.tensor_copy(picked_scales[:], scale_rows[:].bitcast(U8).indirect(offsets[:]))
         for quad in range(4):
             nc.sync.dma_start(
                 out=tab_planes[32 * quad : 32 * quad + 4, :],
                 in_=picked_scales[8 * quad : 8 * quad + 8, :].bitcast(I32),
             )
-        raw_x1 = [load("raw_x10", x[rows(0), cols(1)])]
-
-        quantise(("w", 0, 0), raw_w[0][:, :, cols(0)], both("raw_x11", "table"))
-        raw_x1.append(load("raw_x11", x[rows(1), cols(1)]))
-        table = tile("table", [P, T], I32)
-        nc.sync.dma_start(out=table[:], in_=tab_words[0].rearrange("p t b -> p (t b)").bitcast(I32))
-        quantise(("w", 1, 0), raw_w[0][:, :, cols(1)], both("raw_v0", "raw_v1"))
-        raw_v = [load("raw_v%d" % a, wv[rows(a), :]) for a in range(2)]
+        raw_v = [load("raw_v0", wv[rows(0), :])]
+        quantise(("w", 0, 0), raw_w[0][:, :, cols(0)], both("raw_v1"))
+        raw_v.append(load("raw_v1", wv[rows(1), :]))
+        quantise(("w", 1, 0), raw_w[0][:, :, cols(1)], both())
         quantise(("w", 0, 1), raw_w[1][:, :, cols(0)], both())
         quantise(("w", 1, 1), raw_w[1][:, :, cols(1)], both())
         quantise(("x", 0, 0), raw_x0[0][:], both())
@@ -191,12 +194,8 @@ def tile_list_mlat_scale_kernel(tc, x, w, tab_words, tab_scales, wv, offs, out_0
         for jh in range(2):
             for mt in range(4):
                 score(mt, jh, staged, True)
-                if mt % 2 == 1:
-                    nc.sync.dma_start(
-                        out=out_0[(mt - 1) * P : (mt + 1) * P, cols(jh)].rearrange("(u p) c -> p u c", p=P),
-                        in_=staged[:, mt - 1 : mt + 1, cols(jh)],
-                    )
-        quantise(("v", 0, 0), raw_v[0][:], [(nc.vector.tensor_copy, "qa_bf31")])
+                nc.sync.dma_start(out=out_0[mt * P : (mt + 1) * P, cols(jh)], in_=staged[:, mt, cols(jh)])
+        quantise(("v", 0, 0), raw_v[0][:], [(nc.vector.tensor_copy, "qa_bf30")])
         quantise(("v", 0, 1), raw_v[1][:], [(nc.vector.tensor_copy, "qa_bf31")])
 
         staged = tile("scores1", [P, 4, J], F32, "raw_w1")
@@ -210,4 +209,7 @@ def tile_list_mlat_scale_kernel(tc, x, w, tab_words, tab_scales, wv, offs, out_0
         for nt in range(N // P):
             for jh in range(2):
                 against_table(keys, nt * P, jh, values[:, nt, :], 1.0, jh == 0)
-            nc.sync.dma_start(out=out_1[nt * P : (nt + 1) * P, :], in_=values[:, nt, :])
+                if nt == 3:
+                    nc.sync.dma_start(out=out_1[nt * P : (nt + 1) * P, cols(jh)], in_=values[:, nt, cols(jh)])
+            if nt < 3:
+                nc.sync.dma_start(out=out_1[nt * P : (nt + 1) * P, :], in_=values[:, nt, :])

@@ -167,6 +167,17 @@ def tile_list_mlat_scale_kernel(tc, x, w, tab_words, tab_scales, wv, offs, out_0
         quantise(("w", 0, 1), raw_w[1][:, :, cols(0)], both())
         quantise(("w", 1, 1), raw_w[1][:, :, cols(1)], both())
         quantise(("x", 0, 0), raw_x0[0][:], both())
+        warm = psum.tile([P, W], F32, name="bank")
+        for t in range(PACK):
+            nc.tensor.matmul_mx(
+                out=warm[:],
+                lhsT=codes["w", 0, 0][:, t * P : (t + 1) * P].bitcast(FP8X4),
+                lhsT_scale=scales["w", 0, 0][:, t * P : (t + 1) * P],
+                rhs=codes["x", 0, 0][:].bitcast(FP8X4),
+                rhs_scale=scales["x", 0, 0][:],
+                start=True,
+                stop=True,
+            )
         quantise(("x", 0, 1), raw_x0[1][:], both())
         quantise(("x", 1, 0), raw_x1[0][:], vector_alone())
         quantise(("x", 1, 1), raw_x1[1][:], vector_alone())

@@ -28,7 +28,7 @@ def tile_list_mlat_scale_kernel(tc, x, w, tab_words, tab_scales, wv, offs, out_0
     with ExitStack() as ctx:
         lists = ctx.enter_context(tc.tile_pool(name="lists", bufs=1))
         keep = ctx.enter_context(tc.tile_pool(name="keep", bufs=1))
-        psum = ctx.enter_context(tc.psum_pool(name="psum", bufs=8))
+        psum = ctx.enter_context(tc.psum_pool(name="psum", bufs=4))
 
         def tile(name, shape, dtype, slot=None):
             return keep.tile(shape, dtype, name=name, tag=slot or name, align_bytes=64)
@@ -47,9 +47,9 @@ def tile_list_mlat_scale_kernel(tc, x, w, tab_words, tab_scales, wv, offs, out_0
         codes = {}
         scales = {}
 
-        def quantise(key, src, shares):
+        def quantise(key, src, shares, codes_slot=None):
             name = "%s%d%d" % key
-            codes[key] = tile("codes_" + name, [P, W], U32)
+            codes[key] = tile("codes_" + name, [P, W], U32, codes_slot)
             scales[key] = tile("scales_" + name, [P, W], U8)
             width = W // len(shares)
 
@@ -79,38 +79,52 @@ def tile_list_mlat_scale_kernel(tc, x, w, tab_words, tab_scales, wv, offs, out_0
         def vector_alone():
             return [(nc.vector.tensor_copy, None), (nc.vector.tensor_copy, None)]
 
-        def project(pair, b, slot=None):
+        banks = {}
+
+        def project_passes(pair, b, u, steps):
+            h = pair // 2
+            m0 = (pair % 2) * 2 * P + u * P
+            if (pair, b, u) not in banks:
+                banks[pair, b, u] = psum.tile([P, W], F32, name="qa_bank")
+            for t, a in steps:
+                nc.tensor.matmul_mx(
+                    out=banks[pair, b, u][:, t * P : (t + 1) * P],
+                    lhsT=codes["w", b, a][:, t * P : (t + 1) * P].bitcast(FP8X4),
+                    lhsT_scale=scales["w", b, a][:, t * P : (t + 1) * P],
+                    rhs=codes["x", h, a][:, m0 : m0 + P].bitcast(FP8X4),
+                    rhs_scale=scales["x", h, a][:, m0 : m0 + P],
+                    start=(a == 0 and t == 0),
+                    stop=(a == 1 and t == PACK - 1),
+                )
+
+        def project(pair, b, slot=None, defer=False):
             h = pair // 2
             qa_bf = tile("qa_bf%d%d" % (pair, b), [P, 2 * W], BF16, slot)
             for u in range(2):
-                m0 = (pair % 2) * 2 * P + u * P
-                bank = psum.tile([P, W], F32, name="bank")
-                for t in range(PACK):
-                    for a in range(2):
-                        nc.tensor.matmul_mx(
-                            out=bank[:, t * P : (t + 1) * P],
-                            lhsT=codes["w", b, a][:, t * P : (t + 1) * P].bitcast(FP8X4),
-                            lhsT_scale=scales["w", b, a][:, t * P : (t + 1) * P],
-                            rhs=codes["x", h, a][:, m0 : m0 + P].bitcast(FP8X4),
-                            rhs_scale=scales["x", h, a][:, m0 : m0 + P],
-                            start=(a == 0),
-                            stop=(a == 1),
-                        )
+                first = 1 if (pair, b, u) in banks else 0
+                project_passes(pair, b, u, [(t, a) for t in range(PACK) for a in range(first, 2)])
+                bank = banks[pair, b, u]
                 nc.scalar.copy(
                     out=qa_bf[:, u * W : (u + 1) * W].rearrange("p (m t) -> p m t", t=PACK),
                     in_=bank[:].rearrange("p (t m) -> p m t", t=PACK),
                 )
             part = slice((pair % 2) * 2 * P, (pair % 2 + 1) * 2 * P)
-            nc.vector.quantize_mx(
-                out=codes["q", h, b][:, part].bitcast(FP8X4), scales=scales["q", h, b][:, part], in_=qa_bf[:]
-            )
+
+            def quantise_qa():
+                nc.vector.quantize_mx(
+                    out=codes["q", h, b][:, part].bitcast(FP8X4), scales=scales["q", h, b][:, part], in_=qa_bf[:]
+                )
+
+            if defer:
+                return quantise_qa
+            quantise_qa()
 
         parted = {}
 
-        def pick_words(jh, slot):
+        def pick_words(jh, slot, parted_slot=None):
             picked = tile("picked%d" % jh, [P, W], U32, slot)
             nc.vector.tensor_copy(picked[:], table[:].bitcast(U32).indirect(offsets[:, jh * W // 16 : (jh + 1) * W // 16]))
-            parted[jh] = tile("parted%d" % jh, [P, 2, 2 * W], U8)
+            parted[jh] = tile("parted%d" % jh, [P, 2, 2 * W], U8, parted_slot)
             nc.vector.tensor_copy(
                 out=parted[jh][:].bitcast(U16),
                 in_=picked[:].bitcast(U16).rearrange("p (j d) -> p d j", d=2),
@@ -149,7 +163,6 @@ def tile_list_mlat_scale_kernel(tc, x, w, tab_words, tab_scales, wv, offs, out_0
         nc.vector.memset(tab_planes[:], 0)
         raw_w = [load("raw_w%d" % a, w[rows(a), :]) for a in range(2)]
         raw_x0 = [load("raw_x0%d" % a, x[rows(a), cols(0)]) for a in range(2)]
-
         raw_x1 = [load("raw_x1%d" % a, x[rows(a), cols(1)]) for a in range(2)]
         table = tile("table", [P, T], I32)
         nc.sync.dma_start(out=table[:], in_=tab_words[0].rearrange("p t b -> p (t b)").bitcast(I32))
@@ -167,17 +180,9 @@ def tile_list_mlat_scale_kernel(tc, x, w, tab_words, tab_scales, wv, offs, out_0
         quantise(("w", 0, 1), raw_w[1][:, :, cols(0)], both())
         quantise(("w", 1, 1), raw_w[1][:, :, cols(1)], both())
         quantise(("x", 0, 0), raw_x0[0][:], both())
-        warm = psum.tile([P, W], F32, name="bank")
-        for t in range(PACK):
-            nc.tensor.matmul_mx(
-                out=warm[:],
-                lhsT=codes["w", 0, 0][:, t * P : (t + 1) * P].bitcast(FP8X4),
-                lhsT_scale=scales["w", 0, 0][:, t * P : (t + 1) * P],
-                rhs=codes["x", 0, 0][:].bitcast(FP8X4),
-                rhs_scale=scales["x", 0, 0][:],
-                start=True,
-                stop=True,
-            )
+        for b in range(2):
+            for u in range(2):
+                project_passes(0, b, u, [(t, 0) for t in range(PACK)])
         quantise(("x", 0, 1), raw_x0[1][:], both())
         quantise(("x", 1, 0), raw_x1[0][:], vector_alone())
         quantise(("x", 1, 1), raw_x1[1][:], vector_alone())
@@ -192,14 +197,13 @@ def tile_list_mlat_scale_kernel(tc, x, w, tab_words, tab_scales, wv, offs, out_0
         project(0, 1)
         project(1, 0)
         project(1, 1, "pick_slot")
-        pick_words(0, "pick_slot")
+        late = [project(pair, b, None, True) for pair in (2, 3) for b in range(2)]
+        pick_words(0, "pick_slot", "codes_w01")
         pick_words(1, "pick_slot")
         qa_operand(1, 0, "pick_slot")
         qa_operand(1, 1, "table")
-        project(2, 0)
-        project(2, 1)
-        project(3, 0)
-        project(3, 1)
+        for quantise_later in late:
+            quantise_later()
 
         staged = tile("scores0", [P, 4, J], F32, "raw_w0")
         for jh in range(2):

@@ -28,7 +28,7 @@ def tile_list_mlat_scale_kernel(tc, x, w, tab_words, tab_scales, wv, offs, out_0
     with ExitStack() as ctx:
         lists = ctx.enter_context(tc.tile_pool(name="lists", bufs=1))
         keep = ctx.enter_context(tc.tile_pool(name="keep", bufs=1))
-        psum = ctx.enter_context(tc.psum_pool(name="psum", bufs=4))
+        psum = ctx.enter_context(tc.psum_pool(name="psum", bufs=8))
 
         def tile(name, shape, dtype, slot=None):
             return keep.tile(shape, dtype, name=name, tag=slot or name, align_bytes=64)
@@ -73,11 +73,23 @@ def tile_list_mlat_scale_kernel(tc, x, w, tab_words, tab_scales, wv, offs, out_0
                 part = slice(s * width, (s + 1) * width)
                 nc.vector.quantize_mx(out=codes[key][:, part].bitcast(FP8X4), scales=scales[key][:, part], in_=dst[:])
 
+        def operand(key):
+            name = "%s%d%d" % key
+            codes[key] = tile("codes_" + name, [P, W], U32)
+            scales[key] = tile("scales_" + name, [P, W], U8)
+
+        def cast_half(copy, dst, raw, s):
+            copy(
+                out=dst.rearrange("p (c i j) -> p c j i", i=4, j=PACK),
+                in_=raw[:, :, s * HALF : (s + 1) * HALF].rearrange("p j (c i) -> p c j i", i=4),
+            )
+
+        def quantise_half(key, s, src):
+            part = slice(s * HALF, (s + 1) * HALF)
+            nc.vector.quantize_mx(out=codes[key][:, part].bitcast(FP8X4), scales=scales[key][:, part], in_=src)
+
         def both(vector_slot=None, scalar_slot=None):
             return [(nc.vector.tensor_copy, vector_slot), (nc.scalar.copy, scalar_slot)]
-
-        def vector_alone():
-            return [(nc.vector.tensor_copy, None), (nc.vector.tensor_copy, None)]
 
         banks = {}
 
@@ -85,7 +97,7 @@ def tile_list_mlat_scale_kernel(tc, x, w, tab_words, tab_scales, wv, offs, out_0
             h = pair // 2
             m0 = (pair % 2) * 2 * P + u * P
             if (pair, b, u) not in banks:
-                banks[pair, b, u] = psum.tile([P, W], F32, name="qa_bank")
+                banks[pair, b, u] = psum.tile([P, W], F32, name="bank")
             for t, a in steps:
                 nc.tensor.matmul_mx(
                     out=banks[pair, b, u][:, t * P : (t + 1) * P],
@@ -97,27 +109,28 @@ def tile_list_mlat_scale_kernel(tc, x, w, tab_words, tab_scales, wv, offs, out_0
                     stop=(a == 1 and t == PACK - 1),
                 )
 
-        def project(pair, b, slot=None, defer=False):
-            h = pair // 2
+        qa_tiles = {}
+
+        def project(pair, b, copies, slot=None):
             qa_bf = tile("qa_bf%d%d" % (pair, b), [P, 2 * W], BF16, slot)
             for u in range(2):
                 first = 1 if (pair, b, u) in banks else 0
                 project_passes(pair, b, u, [(t, a) for t in range(PACK) for a in range(first, 2)])
                 bank = banks[pair, b, u]
-                nc.scalar.copy(
+                copies[u](
                     out=qa_bf[:, u * W : (u + 1) * W].rearrange("p (m t) -> p m t", t=PACK),
                     in_=bank[:].rearrange("p (t m) -> p m t", t=PACK),
                 )
-            part = slice((pair % 2) * 2 * P, (pair % 2 + 1) * 2 * P)
+            qa_tiles[pair, b] = qa_bf
 
-            def quantise_qa():
+        def quantise_qa(pair, slot=None):
+            words = tile("codes_q%d" % pair, [P, 2, HALF], U32, slot)
+            for b in range(2):
+                codes["q", pair, b] = words[:, b, :]
+                scales["q", pair, b] = tile("scales_q%d%d" % (pair, b), [P, HALF], U8)
                 nc.vector.quantize_mx(
-                    out=codes["q", h, b][:, part].bitcast(FP8X4), scales=scales["q", h, b][:, part], in_=qa_bf[:]
+                    out=codes["q", pair, b].bitcast(FP8X4), scales=scales["q", pair, b][:], in_=qa_tiles[pair, b][:]
                 )
-
-            if defer:
-                return quantise_qa
-            quantise_qa()
 
         parted = {}
 
@@ -148,8 +161,8 @@ def tile_list_mlat_scale_kernel(tc, x, w, tab_words, tab_scales, wv, offs, out_0
                 nc.vector.tensor_scalar_mul(out=result[:, cols(jh)], in0=bank[:], scalar1=factor)
 
         def score(mt, jh, staged, on_scalar):
-            keys = [("q", mt // 4, b) for b in range(2)]
-            against_table(keys, (mt % 4) * P, jh, staged[:, mt % 4, :], SCORE_SCALE, on_scalar)
+            keys = [("q", mt // 2, b) for b in range(2)]
+            against_table(keys, (mt % 2) * P, jh, staged[:, mt % 4, :], SCORE_SCALE, on_scalar)
 
         offsets = lists.tile([P, J // 16], U16, name="offsets")
         scale_rows = tile("scale_rows", [P, T // 4], I32, "raw_v0")
@@ -163,7 +176,6 @@ def tile_list_mlat_scale_kernel(tc, x, w, tab_words, tab_scales, wv, offs, out_0
         nc.vector.memset(tab_planes[:], 0)
         raw_w = [load("raw_w%d" % a, w[rows(a), :]) for a in range(2)]
         raw_x0 = [load("raw_x0%d" % a, x[rows(a), cols(0)]) for a in range(2)]
-        raw_x1 = [load("raw_x1%d" % a, x[rows(a), cols(1)]) for a in range(2)]
         table = tile("table", [P, T], I32)
         nc.sync.dma_start(out=table[:], in_=tab_words[0].rearrange("p t b -> p (t b)").bitcast(I32))
 
@@ -174,9 +186,11 @@ def tile_list_mlat_scale_kernel(tc, x, w, tab_words, tab_scales, wv, offs, out_0
                 in_=picked_scales[8 * quad : 8 * quad + 8, :].bitcast(I32),
             )
         raw_v = [load("raw_v0", wv[rows(0), :])]
-        quantise(("w", 0, 0), raw_w[0][:, :, cols(0)], both("raw_v1"))
+        quantise(("w", 0, 0), raw_w[0][:, :, cols(0)], both("raw_v1", "raw_x10"))
         raw_v.append(load("raw_v1", wv[rows(1), :]))
-        quantise(("w", 1, 0), raw_w[0][:, :, cols(1)], both())
+        raw_x1 = [load("raw_x10", x[rows(0), cols(1)])]
+        quantise(("w", 1, 0), raw_w[0][:, :, cols(1)], both(None, "raw_x11"))
+        raw_x1.append(load("raw_x11", x[rows(1), cols(1)]))
         quantise(("w", 0, 1), raw_w[1][:, :, cols(0)], both())
         quantise(("w", 1, 1), raw_w[1][:, :, cols(1)], both())
         quantise(("x", 0, 0), raw_x0[0][:], both())
@@ -184,47 +198,96 @@ def tile_list_mlat_scale_kernel(tc, x, w, tab_words, tab_scales, wv, offs, out_0
             for u in range(2):
                 project_passes(0, b, u, [(t, 0) for t in range(PACK)])
         quantise(("x", 0, 1), raw_x0[1][:], both())
-        quantise(("x", 1, 0), raw_x1[0][:], vector_alone())
-        quantise(("x", 1, 1), raw_x1[1][:], vector_alone())
 
-        def qa_operand(h, b, slot):
-            codes["q", h, b] = tile("codes_q%d%d" % (h, b), [P, W], U32, slot)
-            scales["q", h, b] = tile("scales_q%d%d" % (h, b), [P, W], U8)
+        on_scalar = [nc.scalar.copy, nc.scalar.copy]
+        on_vector = [nc.vector.tensor_copy, nc.vector.tensor_copy]
+        on_both = [nc.scalar.copy, nc.vector.tensor_copy]
+        project(0, 0, on_both)
+        project(0, 1, on_both, "gather_slot")
+        quantise_qa(0)
+        project(1, 0, on_scalar, "vector_chain")
+        project(1, 1, on_scalar)
+        for t in range(3):
+            nc.tensor.matmul_mx(
+                out=banks[0, 0, 0][:],
+                lhsT=codes["w", 0, 0][:, t * P : (t + 1) * P].bitcast(FP8X4),
+                lhsT_scale=scales["w", 0, 0][:, t * P : (t + 1) * P],
+                rhs=table[:, 0:HALF].bitcast(FP4X4),
+                rhs_scale=scales["x", 0, 0][:],
+                start=True,
+                stop=True,
+            )
+        pick_words(0, "gather_slot")
+        quantise_qa(1, "gather_slot")
+        pick_words(1, "vector_chain")
 
-        qa_operand(0, 0, "grouped_x11_0")
-        qa_operand(0, 1, "grouped_x11_1")
-        project(0, 0)
-        project(0, 1)
-        project(1, 0)
-        project(1, 1, "pick_slot")
-        late = [project(pair, b, None, True) for pair in (2, 3) for b in range(2)]
-        pick_words(0, "pick_slot", "codes_w01")
-        pick_words(1, "pick_slot")
-        qa_operand(1, 0, "pick_slot")
-        qa_operand(1, 1, "table")
-        for quantise_later in late:
-            quantise_later()
+        for a in range(2):
+            operand(("v", 0, a))
+            operand(("x", 1, a))
+        grouped_v0 = tile("grouped_v0", [P, 2, 2 * W], BF16, "qa_bf11")
+        for s in range(2):
+            cast_half(nc.scalar.copy, grouped_v0[:, s, :], raw_v[0], s)
+        for s in range(2):
+            grouped_v1 = tile("grouped_v1%d" % s, [P, 2 * W], BF16, "vector_chain")
+            cast_half(nc.vector.tensor_copy, grouped_v1[:], raw_v[1], s)
+            quantise_half(("v", 0, 0), s, grouped_v0[:, s, :])
+            quantise_half(("v", 0, 1), s, grouped_v1[:])
+        for s in range(2):
+            grouped_x1 = tile("grouped_x1%d" % s, [P, 2, 2 * W], BF16, "vector_chain")
+            for a in range(2):
+                cast_half(nc.vector.tensor_copy, grouped_x1[:, a, :], raw_x1[a], s)
+            for a in range(2):
+                quantise_half(("x", 1, a), s, grouped_x1[:, a, :])
 
-        staged = tile("scores0", [P, 4, J], F32, "raw_w0")
-        for jh in range(2):
-            for mt in range(4):
-                score(mt, jh, staged, True)
-                nc.sync.dma_start(out=out_0[mt * P : (mt + 1) * P, cols(jh)], in_=staged[:, mt, cols(jh)])
-        quantise(("v", 0, 0), raw_v[0][:], [(nc.vector.tensor_copy, "qa_bf30")])
-        quantise(("v", 0, 1), raw_v[1][:], [(nc.vector.tensor_copy, "qa_bf31")])
-
-        staged = tile("scores1", [P, 4, J], F32, "raw_w1")
-        for mt in range(4, 8):
+        staged = tile("scores0", [P, 4, J], F32, "raw_v0")
+        for mt in range(4):
             score(mt, 0, staged, True)
-            score(mt, 1, staged, mt == 4)
-            nc.sync.dma_start(out=out_0[mt * P : (mt + 1) * P, :], in_=staged[:, mt % 4, :])
+        nc.sync.dma_start(out=out_0[0:W, cols(0)].rearrange("(u p) c -> p u c", p=P), in_=staged[:, :, cols(0)])
+        for mt in range(4):
+            score(mt, 1, staged, True)
+            if mt % 2 == 1:
+                nc.sync.dma_start(
+                    out=out_0[(mt - 1) * P : (mt + 1) * P, cols(1)].rearrange("(u p) c -> p u c", p=P),
+                    in_=staged[:, mt - 1 : mt + 1, cols(1)],
+                )
 
-        values = tile("values", [P, 4, J], F32, "table")
+        values = tile("values", [P, 4, J], F32, "raw_w1")
         keys = [("v", 0, a) for a in range(2)]
         for nt in range(N // P):
             for jh in range(2):
-                against_table(keys, nt * P, jh, values[:, nt, :], 1.0, jh == 0)
-                if nt == 3:
-                    nc.sync.dma_start(out=out_1[nt * P : (nt + 1) * P, cols(jh)], in_=values[:, nt, cols(jh)])
-            if nt < 3:
-                nc.sync.dma_start(out=out_1[nt * P : (nt + 1) * P, :], in_=values[:, nt, :])
+                against_table(keys, nt * P, jh, values[:, nt, :], 1.0, True)
+            nc.sync.dma_start(out=out_1[nt * P : (nt + 1) * P, :], in_=values[:, nt, :])
+
+        project(2, 0, on_vector)
+        project(2, 1, on_vector)
+        quantise_qa(2)
+        project(3, 0, on_scalar)
+        project(3, 1, on_scalar)
+        quantise_qa(3)
+
+        staged = tile("scores1", [P, 4, J], F32, "raw_w0")
+        for mt in range(4, 8):
+            for jh in range(2):
+                if (mt, jh) != (7, 1):
+                    score(mt, jh, staged, jh == 0)
+                    nc.sync.dma_start(out=out_0[mt * P : (mt + 1) * P, cols(jh)], in_=staged[:, mt % 4, cols(jh)])
+        for s in range(2):
+            bank = psum.tile([P, W], F32, name="bank")
+            for c0 in (0, P):
+                j0 = s * HALF + c0
+                for b in range(2):
+                    nc.tensor.matmul_mx(
+                        out=bank[:, c0 : c0 + P],
+                        lhsT=codes["q", 3, b][:, P : 2 * P].bitcast(FP8X4),
+                        lhsT_scale=scales["q", 3, b][:, P : 2 * P],
+                        rhs=parted[1][:, b, 2 * j0 : 2 * (j0 + P)].bitcast(FP4X4),
+                        rhs_scale=tab_planes[:].bitcast(U8)[:, b * J + W + j0 : b * J + W + j0 + P],
+                        start=(b == 0),
+                        stop=(b == 1),
+                    )
+            last = slice(W + s * HALF, W + (s + 1) * HALF)
+            if s == 0:
+                nc.vector.tensor_scalar_mul(out=staged[:, 3, last], in0=bank[:, 0:HALF], scalar1=SCORE_SCALE)
+            else:
+                nc.scalar.activation(out=staged[:, 3, last], in_=bank[:, 0:HALF], func=COPY, scale=SCORE_SCALE)
+            nc.sync.dma_start(out=out_0[M - P : M, last], in_=staged[:, 3, last])

@@ -192,6 +192,17 @@ def tile_list_mlat_scale_kernel(tc, x, w, tab_words, tab_scales, wv, offs, out_0
         quantise(("w", 1, 0), raw_w[0][:, :, cols(1)], both(None, "raw_x11"))
         raw_x1.append(load("raw_x11", x[rows(1), cols(1)]))
         quantise(("w", 0, 1), raw_w[1][:, :, cols(0)], both())
+        warm = psum.tile([P, W], F32, name="bank")
+        for t in range(PACK):
+            nc.tensor.matmul_mx(
+                out=warm[:],
+                lhsT=codes["w", 0, 1][:, t * P : (t + 1) * P].bitcast(FP8X4),
+                lhsT_scale=scales["w", 0, 1][:, t * P : (t + 1) * P],
+                rhs=codes["w", 0, 0][:].bitcast(FP8X4),
+                rhs_scale=scales["w", 0, 0][:],
+                start=True,
+                stop=True,
+            )
         quantise(("w", 1, 1), raw_w[1][:, :, cols(1)], both())
         quantise(("x", 0, 0), raw_x0[0][:], both())
         for b in range(2):
@@ -268,26 +279,5 @@ def tile_list_mlat_scale_kernel(tc, x, w, tab_words, tab_scales, wv, offs, out_0
         staged = tile("scores1", [P, 4, J], F32, "raw_w0")
         for mt in range(4, 8):
             for jh in range(2):
-                if (mt, jh) != (7, 1):
-                    score(mt, jh, staged, jh == 0)
-                    nc.sync.dma_start(out=out_0[mt * P : (mt + 1) * P, cols(jh)], in_=staged[:, mt % 4, cols(jh)])
-        for s in range(2):
-            bank = psum.tile([P, W], F32, name="bank")
-            for c0 in (0, P):
-                j0 = s * HALF + c0
-                for b in range(2):
-                    nc.tensor.matmul_mx(
-                        out=bank[:, c0 : c0 + P],
-                        lhsT=codes["q", 3, b][:, P : 2 * P].bitcast(FP8X4),
-                        lhsT_scale=scales["q", 3, b][:, P : 2 * P],
-                        rhs=parted[1][:, b, 2 * j0 : 2 * (j0 + P)].bitcast(FP4X4),
-                        rhs_scale=tab_planes[:].bitcast(U8)[:, b * J + W + j0 : b * J + W + j0 + P],
-                        start=(b == 0),
-                        stop=(b == 1),
-                    )
-            last = slice(W + s * HALF, W + (s + 1) * HALF)
-            if s == 0:
-                nc.vector.tensor_scalar_mul(out=staged[:, 3, last], in0=bank[:, 0:HALF], scalar1=SCORE_SCALE)
-            else:
-                nc.scalar.activation(out=staged[:, 3, last], in_=bank[:, 0:HALF], func=COPY, scale=SCORE_SCALE)
-            nc.sync.dma_start(out=out_0[M - P : M, last], in_=staged[:, 3, last])
+                score(mt, jh, staged, jh == 0)
+                nc.sync.dma_start(out=out_0[mt * P : (mt + 1) * P, cols(jh)], in_=staged[:, mt % 4, cols(jh)])

@@ -134,9 +134,23 @@ def tile_list_mlat_scale_kernel(tc, x, w, tab_words, tab_scales, wv, offs, out_0
 
         parted = {}
 
+        def keep_warm(words):
+            for t in range(2):
+                nc.tensor.matmul_mx(
+                    out=banks[0, 0, 0][:],
+                    lhsT=codes["w", 0, 0][:, t * P : (t + 1) * P].bitcast(FP8X4),
+                    lhsT_scale=scales["w", 0, 0][:, t * P : (t + 1) * P],
+                    rhs=words.bitcast(FP4X4),
+                    rhs_scale=scales["x", 0, 0][:],
+                    start=True,
+                    stop=True,
+                )
+
         def pick_words(jh, slot, parted_slot=None):
             picked = tile("picked%d" % jh, [P, W], U32, slot)
             nc.vector.tensor_copy(picked[:], table[:].bitcast(U32).indirect(offsets[:, jh * W // 16 : (jh + 1) * W // 16]))
+            if jh == 0:
+                keep_warm(picked[:, 0:HALF])
             parted[jh] = tile("parted%d" % jh, [P, 2, 2 * W], U8, parted_slot)
             nc.vector.tensor_copy(
                 out=parted[jh][:].bitcast(U16),
@@ -169,12 +183,12 @@ def tile_list_mlat_scale_kernel(tc, x, w, tab_words, tab_scales, wv, offs, out_0
         picked_scales = tile("picked_scales", [P, J], U8)
         tab_planes = tile("tab_planes", [P, 2 * J // 4], I32)
 
-        nc.sync.dma_start(out=scale_rows[0:32, :], in_=tab_scales.bitcast(I32).rearrange("a q n -> q a n"))
-        nc.sync.dma_start(offsets[:], offs)
-        nc.vector.memset(scale_rows[32:64, :], 0)
-        nc.vector.memset(scale_rows[64:P, :], 0)
+        nc.vector.memset(scale_rows[:], 0)
         nc.vector.memset(tab_planes[:], 0)
-        raw_w = [load("raw_w%d" % a, w[rows(a), :]) for a in range(2)]
+        raw_w = [load("raw_w0", w[rows(0), :])]
+        nc.sync.dma_start(offsets[:], offs)
+        nc.sync.dma_start(out=scale_rows[0:P:4, :], in_=tab_scales.bitcast(I32).rearrange("a q n -> q a n"))
+        raw_w.append(load("raw_w1", w[rows(1), :]))
         raw_x0 = [load("raw_x0%d" % a, x[rows(a), cols(0)]) for a in range(2)]
         table = tile("table", [P, T], I32)
         nc.sync.dma_start(out=table[:], in_=tab_words[0].rearrange("p t b -> p (t b)").bitcast(I32))
@@ -183,7 +197,7 @@ def tile_list_mlat_scale_kernel(tc, x, w, tab_words, tab_scales, wv, offs, out_0
         for quad in range(4):
             nc.sync.dma_start(
                 out=tab_planes[32 * quad : 32 * quad + 4, :],
-                in_=picked_scales[8 * quad : 8 * quad + 8, :].bitcast(I32),
+                in_=picked_scales[32 * quad : 32 * quad + 32 : 4, :].bitcast(I32),
             )
         raw_v = [load("raw_v0", wv[rows(0), :])]
         quantise(("w", 0, 0), raw_w[0][:, :, cols(0)], both("raw_v1", "raw_x10"))
@@ -214,22 +228,13 @@ def tile_list_mlat_scale_kernel(tc, x, w, tab_words, tab_scales, wv, offs, out_0
         on_vector = [nc.vector.tensor_copy, nc.vector.tensor_copy]
         on_both = [nc.scalar.copy, nc.vector.tensor_copy]
         project(0, 0, on_both)
-        project(0, 1, on_both, "gather_slot")
+        project(0, 1, on_both, "vector_chain")
         quantise_qa(0)
-        project(1, 0, on_scalar, "vector_chain")
+        project(1, 0, on_scalar)
         project(1, 1, on_scalar)
-        for t in range(3):
-            nc.tensor.matmul_mx(
-                out=banks[0, 0, 0][:],
-                lhsT=codes["w", 0, 0][:, t * P : (t + 1) * P].bitcast(FP8X4),
-                lhsT_scale=scales["w", 0, 0][:, t * P : (t + 1) * P],
-                rhs=table[:, 0:HALF].bitcast(FP4X4),
-                rhs_scale=scales["x", 0, 0][:],
-                start=True,
-                stop=True,
-            )
-        pick_words(0, "gather_slot")
-        quantise_qa(1, "gather_slot")
+        keep_warm(table[:, 0:HALF])
+        quantise_qa(1)
+        pick_words(0, "vector_chain")
         pick_words(1, "vector_chain")
 
         for a in range(2):
@@ -272,12 +277,12 @@ def tile_list_mlat_scale_kernel(tc, x, w, tab_words, tab_scales, wv, offs, out_0
         project(2, 0, on_vector)
         project(2, 1, on_vector)
         quantise_qa(2)
-        project(3, 0, on_scalar)
-        project(3, 1, on_scalar)
+        project(3, 0, on_both)
+        project(3, 1, on_both)
         quantise_qa(3)
 
         staged = tile("scores1", [P, 4, J], F32, "raw_w0")
         for mt in range(4, 8):
             for jh in range(2):
-                score(mt, jh, staged, jh == 0)
+                score(mt, jh, staged, mt == 4 or jh == 1)
                 nc.sync.dma_start(out=out_0[mt * P : (mt + 1) * P, cols(jh)], in_=staged[:, mt % 4, cols(jh)])

@@ -20,6 +20,7 @@ PACK = 4
 KP = P * PACK
 W = 512
 HALF = W // 2
+EARLY = 3 * HALF
 SCORE_SCALE = 0.03125
 
 
@@ -56,16 +57,10 @@ def tile_list_mlat_scale_kernel(tc, x, w, tab_words, tab_scales, wv, offs, out_0
             def cast(s):
                 copy, slot = shares[s]
                 dst = tile("grouped_%s_%d" % (name, s), [P, width * PACK], BF16, slot)
-                if key[0] == "w":
-                    copy(
-                        out=dst[:].rearrange("p (t m j) -> p m j t", t=2, j=PACK),
-                        in_=src.rearrange("p j (m t) -> p m j t", t=PACK)[:, :, :, 2 * s : 2 * s + 2],
-                    )
-                else:
-                    copy(
-                        out=dst[:].rearrange("p (c i j) -> p c j i", i=4, j=PACK),
-                        in_=src[:, :, s * width : (s + 1) * width].rearrange("p j (c i) -> p c j i", i=4),
-                    )
+                copy(
+                    out=dst[:].rearrange("p (t m j) -> p m j t", t=2, j=PACK),
+                    in_=src.rearrange("p j (m t) -> p m j t", t=PACK)[:, :, :, 2 * s : 2 * s + 2],
+                )
                 return dst
 
             for s in range(len(shares)):
@@ -91,11 +86,19 @@ def tile_list_mlat_scale_kernel(tc, x, w, tab_words, tab_scales, wv, offs, out_0
         def both(vector_slot=None, scalar_slot=None):
             return [(nc.vector.tensor_copy, vector_slot), (nc.scalar.copy, scalar_slot)]
 
+        def quantise_x(a, pair, raw, c0, copy, slot=None):
+            grouped = tile("grouped_x%d%d" % (a, pair), [P, HALF * PACK], BF16, slot)
+            copy(
+                out=grouped[:].rearrange("p (c i j) -> p c j i", i=4, j=PACK),
+                in_=raw[:, :, c0 : c0 + HALF].rearrange("p j (c i) -> p c j i", i=4),
+            )
+            part = slice(pair * HALF, (pair + 1) * HALF)
+            nc.vector.quantize_mx(out=x_codes[a][:, part].bitcast(FP8X4), scales=x_scales[a, pair][:], in_=grouped[:])
+
         banks = {}
 
         def project_passes(pair, b, u, steps):
-            h = pair // 2
-            m0 = (pair % 2) * 2 * P + u * P
+            m0 = pair * HALF + u * P
             if (pair, b, u) not in banks:
                 banks[pair, b, u] = psum.tile([P, W], F32, name="bank")
             for t, a in steps:
@@ -103,8 +106,8 @@ def tile_list_mlat_scale_kernel(tc, x, w, tab_words, tab_scales, wv, offs, out_0
                     out=banks[pair, b, u][:, t * P : (t + 1) * P],
                     lhsT=codes["w", b, a][:, t * P : (t + 1) * P].bitcast(FP8X4),
                     lhsT_scale=scales["w", b, a][:, t * P : (t + 1) * P],
-                    rhs=codes["x", h, a][:, m0 : m0 + P].bitcast(FP8X4),
-                    rhs_scale=scales["x", h, a][:, m0 : m0 + P],
+                    rhs=x_codes[a][:, m0 : m0 + P].bitcast(FP8X4),
+                    rhs_scale=x_scales[a, pair][:, u * P : (u + 1) * P],
                     start=(a == 0 and t == 0),
                     stop=(a == 1 and t == PACK - 1),
                 )
@@ -123,25 +126,27 @@ def tile_list_mlat_scale_kernel(tc, x, w, tab_words, tab_scales, wv, offs, out_0
                 )
             qa_tiles[pair, b] = qa_bf
 
-        def quantise_qa(pair, slot=None):
-            words = tile("codes_q%d" % pair, [P, 2, HALF], U32, slot)
+        def quantise_qa_half(pair, b, slot=None):
+            codes["q", pair, b] = tile("codes_q%d%d" % (pair, b), [P, HALF], U32, slot)
+            scales["q", pair, b] = tile("scales_q%d%d" % (pair, b), [P, HALF], U8)
+            nc.vector.quantize_mx(
+                out=codes["q", pair, b][:].bitcast(FP8X4), scales=scales["q", pair, b][:], in_=qa_tiles[pair, b][:]
+            )
+
+        def quantise_qa(pair):
             for b in range(2):
-                codes["q", pair, b] = words[:, b, :]
-                scales["q", pair, b] = tile("scales_q%d%d" % (pair, b), [P, HALF], U8)
-                nc.vector.quantize_mx(
-                    out=codes["q", pair, b].bitcast(FP8X4), scales=scales["q", pair, b][:], in_=qa_tiles[pair, b][:]
-                )
+                quantise_qa_half(pair, b)
 
         parted = {}
 
-        def keep_warm(words):
-            for t in range(2):
+        def keep_warm(bank, b, c0):
+            for repeat in range(2):
                 nc.tensor.matmul_mx(
-                    out=banks[0, 0, 0][:],
-                    lhsT=codes["w", 0, 0][:, t * P : (t + 1) * P].bitcast(FP8X4),
-                    lhsT_scale=scales["w", 0, 0][:, t * P : (t + 1) * P],
-                    rhs=words.bitcast(FP4X4),
-                    rhs_scale=scales["x", 0, 0][:],
+                    out=bank[:],
+                    lhsT=codes["w", b, 1][:, c0 : c0 + P].bitcast(FP8X4),
+                    lhsT_scale=scales["w", b, 1][:, c0 : c0 + P],
+                    rhs=x_codes[0][:, 0:W].bitcast(FP8X4),
+                    rhs_scale=scales["w", 0, 0][:],
                     start=True,
                     stop=True,
                 )
@@ -150,7 +155,15 @@ def tile_list_mlat_scale_kernel(tc, x, w, tab_words, tab_scales, wv, offs, out_0
             picked = tile("picked%d" % jh, [P, W], U32, slot)
             nc.vector.tensor_copy(picked[:], table[:].bitcast(U32).indirect(offsets[:, jh * W // 16 : (jh + 1) * W // 16]))
             if jh == 0:
-                keep_warm(picked[:, 0:HALF])
+                nc.tensor.matmul_mx(
+                    out=banks[1, 0, 0][:, 0:P],
+                    lhsT=codes["q", 0, 0][:, 0:P].bitcast(FP8X4),
+                    lhsT_scale=x_scales[1, 0][:, 0:P],
+                    rhs=picked[:, 0 : P // 2].bitcast(FP4X4),
+                    rhs_scale=x_scales[1, 0][:, P:HALF],
+                    start=True,
+                    stop=True,
+                )
             parted[jh] = tile("parted%d" % jh, [P, 2, 2 * W], U8, parted_slot)
             nc.vector.tensor_copy(
                 out=parted[jh][:].bitcast(U16),
@@ -182,17 +195,25 @@ def tile_list_mlat_scale_kernel(tc, x, w, tab_words, tab_scales, wv, offs, out_0
         scale_rows = tile("scale_rows", [P, T // 4], I32, "raw_v0")
         picked_scales = tile("picked_scales", [P, J], U8)
         tab_planes = tile("tab_planes", [P, 2 * J // 4], I32)
+        x_codes = [tile("x_codes%d" % a, [P, M], U32) for a in range(2)]
+        x_scales = {(a, pair): tile("x_scales%d%d" % (a, pair), [P, HALF], U8) for pair in range(4) for a in range(2)}
+        on_scalar = [nc.scalar.copy, nc.scalar.copy]
+        on_both = [nc.scalar.copy, nc.vector.tensor_copy]
+        early_casts = [nc.vector.tensor_copy, nc.scalar.copy, nc.vector.tensor_copy]
 
         nc.vector.memset(scale_rows[:], 0)
         nc.vector.memset(tab_planes[:], 0)
-        raw_w = [load("raw_w0", w[rows(0), :])]
+        early_x = [load("early_x0", x[rows(0), 0:EARLY])]
         nc.sync.dma_start(offsets[:], offs)
         nc.sync.dma_start(out=scale_rows[0:P:4, :], in_=tab_scales.bitcast(I32).rearrange("a q n -> q a n"))
-        raw_w.append(load("raw_w1", w[rows(1), :]))
-        raw_x0 = [load("raw_x0%d" % a, x[rows(a), cols(0)]) for a in range(2)]
+        raw_w = [load("raw_w%d" % a, w[rows(a), :]) for a in range(2)]
+        first_x1 = load("first_x1", x[rows(1), 0:W])
+        third_x1 = load("third_x1", x[rows(1), W:EARLY])
         table = tile("table", [P, T], I32)
         nc.sync.dma_start(out=table[:], in_=tab_words[0].rearrange("p t b -> p (t b)").bitcast(I32))
 
+        for pair in range(3):
+            quantise_x(0, pair, early_x[0], pair * HALF, early_casts[pair])
         nc.vector.tensor_copy(picked_scales[:], scale_rows[:].bitcast(U8).indirect(offsets[:]))
         for quad in range(4):
             nc.sync.dma_start(
@@ -200,62 +221,51 @@ def tile_list_mlat_scale_kernel(tc, x, w, tab_words, tab_scales, wv, offs, out_0
                 in_=picked_scales[32 * quad : 32 * quad + 32 : 4, :].bitcast(I32),
             )
         raw_v = [load("raw_v0", wv[rows(0), :])]
-        quantise(("w", 0, 0), raw_w[0][:, :, cols(0)], both("raw_v1", "raw_x10"))
+        quantise(("w", 0, 0), raw_w[0][:, :, cols(0)], both("raw_v1", "late_x0"))
         raw_v.append(load("raw_v1", wv[rows(1), :]))
-        raw_x1 = [load("raw_x10", x[rows(0), cols(1)])]
-        quantise(("w", 1, 0), raw_w[0][:, :, cols(1)], both(None, "raw_x11"))
-        raw_x1.append(load("raw_x11", x[rows(1), cols(1)]))
-        quantise(("w", 0, 1), raw_w[1][:, :, cols(0)], both())
-        warm = psum.tile([P, W], F32, name="bank")
-        for t in range(PACK):
-            nc.tensor.matmul_mx(
-                out=warm[:],
-                lhsT=codes["w", 0, 1][:, t * P : (t + 1) * P].bitcast(FP8X4),
-                lhsT_scale=scales["w", 0, 1][:, t * P : (t + 1) * P],
-                rhs=codes["w", 0, 0][:].bitcast(FP8X4),
-                rhs_scale=scales["w", 0, 0][:],
-                start=True,
-                stop=True,
-            )
-        quantise(("w", 1, 1), raw_w[1][:, :, cols(1)], both())
-        quantise(("x", 0, 0), raw_x0[0][:], both())
-        for b in range(2):
-            for u in range(2):
-                project_passes(0, b, u, [(t, 0) for t in range(PACK)])
-        quantise(("x", 0, 1), raw_x0[1][:], both())
+        late_x = [load("late_x0", x[rows(0), EARLY:M])]
+        quantise(("w", 1, 0), raw_w[0][:, :, cols(1)], both(None, "late_x1"))
+        late_x.append(load("late_x1", x[rows(1), EARLY:M]))
 
-        on_scalar = [nc.scalar.copy, nc.scalar.copy]
-        on_vector = [nc.vector.tensor_copy, nc.vector.tensor_copy]
-        on_both = [nc.scalar.copy, nc.vector.tensor_copy]
+        first_banks = [(pair, b, u) for pair in range(2) for b in range(2) for u in range(2)]
+        for pair, b, u in first_banks[:-1]:
+            project_passes(pair, b, u, [(t, 0) for t in range(PACK)])
+        warm = psum.tile([P, W], F32, name="bank")
+        for b in range(2):
+            quantise(("w", b, 1), raw_w[1][:, :, cols(b)], both())
+            keep_warm(warm, b, 0)
+        keep_warm(warm, 1, HALF)
+        project_passes(1, 1, 1, [(t, 0) for t in range(PACK)])
+        for pair in range(2):
+            quantise_x(1, pair, first_x1, pair * HALF, early_casts[pair])
+        quantise_x(1, 2, third_x1, 0, early_casts[2])
+
         project(0, 0, on_both)
-        project(0, 1, on_both, "vector_chain")
+        project(0, 1, on_both, "first_chain")
         quantise_qa(0)
         project(1, 0, on_scalar)
         project(1, 1, on_scalar)
-        keep_warm(table[:, 0:HALF])
-        quantise_qa(1)
-        pick_words(0, "vector_chain")
-        pick_words(1, "vector_chain")
+        project(2, 0, on_scalar, "after_q20")
+        project(2, 1, on_scalar, "after_q2")
+        quantise_qa_half(1, 0)
+        pick_words(0, "first_chain")
+        quantise_qa_half(1, 1, "x_scales10")
+        pick_words(1, "first_chain")
+        quantise_qa_half(2, 0, "first_chain")
+        quantise_qa_half(2, 1, "after_q20")
 
         for a in range(2):
             operand(("v", 0, a))
-            operand(("x", 1, a))
-        grouped_v0 = tile("grouped_v0", [P, 2, 2 * W], BF16, "qa_bf11")
         for s in range(2):
-            cast_half(nc.scalar.copy, grouped_v0[:, s, :], raw_v[0], s)
-        for s in range(2):
-            grouped_v1 = tile("grouped_v1%d" % s, [P, 2 * W], BF16, "vector_chain")
-            cast_half(nc.vector.tensor_copy, grouped_v1[:], raw_v[1], s)
-            quantise_half(("v", 0, 0), s, grouped_v0[:, s, :])
-            quantise_half(("v", 0, 1), s, grouped_v1[:])
-        for s in range(2):
-            grouped_x1 = tile("grouped_x1%d" % s, [P, 2, 2 * W], BF16, "vector_chain")
+            grouped_v = tile("grouped_v%d" % s, [P, 2, 2 * W], BF16, None if s else "after_q2")
             for a in range(2):
-                cast_half(nc.vector.tensor_copy, grouped_x1[:, a, :], raw_x1[a], s)
+                cast_half(nc.vector.tensor_copy, grouped_v[:, a, :], raw_v[a], s)
             for a in range(2):
-                quantise_half(("x", 1, a), s, grouped_x1[:, a, :])
+                quantise_half(("v", 0, a), s, grouped_v[:, a, :])
+        for a in range(2):
+            quantise_x(a, 3, late_x[a], 0, nc.vector.tensor_copy)
 
-        staged = tile("scores0", [P, 4, J], F32, "raw_v0")
+        staged = tile("scores0", [P, 4, J], F32, "raw_w1")
         for mt in range(4):
             score(mt, 0, staged, True)
         nc.sync.dma_start(out=out_0[0:W, cols(0)].rearrange("(u p) c -> p u c", p=P), in_=staged[:, :, cols(0)])
@@ -266,23 +276,27 @@ def tile_list_mlat_scale_kernel(tc, x, w, tab_words, tab_scales, wv, offs, out_0
                     out=out_0[(mt - 1) * P : (mt + 1) * P, cols(1)].rearrange("(u p) c -> p u c", p=P),
                     in_=staged[:, mt - 1 : mt + 1, cols(1)],
                 )
+        staged = tile("scores1", [P, 4, J], F32, "raw_w0")
+        for mt in range(4, 6):
+            for jh in range(2):
+                score(mt, jh, staged, True)
+            nc.sync.dma_start(out=out_0[mt * P : (mt + 1) * P, :], in_=staged[:, mt % 4, :])
 
-        values = tile("values", [P, 4, J], F32, "raw_w1")
+        values = tile("values", [P, 4, J], F32)
         keys = [("v", 0, a) for a in range(2)]
-        for nt in range(N // P):
+        for nt in range(2):
             for jh in range(2):
                 against_table(keys, nt * P, jh, values[:, nt, :], 1.0, True)
             nc.sync.dma_start(out=out_1[nt * P : (nt + 1) * P, :], in_=values[:, nt, :])
 
-        project(2, 0, on_vector)
-        project(2, 1, on_vector)
-        quantise_qa(2)
         project(3, 0, on_both)
         project(3, 1, on_both)
         quantise_qa(3)
-
-        staged = tile("scores1", [P, 4, J], F32, "raw_w0")
-        for mt in range(4, 8):
+        for nt in range(2, 4):
             for jh in range(2):
-                score(mt, jh, staged, mt == 4 or jh == 1)
+                against_table(keys, nt * P, jh, values[:, nt, :], 1.0, True)
+                nc.sync.dma_start(out=out_1[nt * P : (nt + 1) * P, cols(jh)], in_=values[:, nt, cols(jh)])
+        for mt in range(6, 8):
+            for jh in range(2):
+                score(mt, jh, staged, jh == 1)
                 nc.sync.dma_start(out=out_0[mt * P : (mt + 1) * P, cols(jh)], in_=staged[:, mt % 4, cols(jh)])

@@ -75,9 +75,12 @@ def tile_list_mlat_scale_kernel(tc, x, w, tab_words, tab_scales, wv, offs, out_0
 
         def cast_half(copy, dst, raw, s):
             copy(
-                out=dst.rearrange("p (c i j) -> p c j i", i=4, j=PACK),
-                in_=raw[:, :, s * HALF : (s + 1) * HALF].rearrange("p j (c i) -> p c j i", i=4),
+                out=dst.rearrange("p (e c i j) -> p c j i e", e=2, i=2, j=PACK),
+                in_=raw[:, :, s * HALF : (s + 1) * HALF].rearrange("p j (c i e) -> p c j i e", i=2, e=2),
             )
+
+        def paired_rows(out, pair):
+            return out[pair * HALF : (pair + 1) * HALF, :].rearrange("(p e) c -> p e c", e=2)
 
         def quantise_half(key, s, src):
             part = slice(s * HALF, (s + 1) * HALF)
@@ -121,8 +124,8 @@ def tile_list_mlat_scale_kernel(tc, x, w, tab_words, tab_scales, wv, offs, out_0
                 project_passes(pair, b, u, [(t, a) for t in range(PACK) for a in range(first, 2)])
                 bank = banks[pair, b, u]
                 copies[u](
-                    out=qa_bf[:, u * W : (u + 1) * W].rearrange("p (m t) -> p m t", t=PACK),
-                    in_=bank[:].rearrange("p (t m) -> p m t", t=PACK),
+                    out=qa_bf[:].rearrange("p (e u q t) -> p u e q t", e=2, u=2, t=PACK)[:, u],
+                    in_=bank[:].rearrange("p (t q e) -> p e q t", t=PACK, e=2),
                 )
             qa_tiles[pair, b] = qa_bf
 
@@ -268,26 +271,22 @@ def tile_list_mlat_scale_kernel(tc, x, w, tab_words, tab_scales, wv, offs, out_0
         staged = tile("scores0", [P, 4, J], F32, "raw_w1")
         for mt in range(4):
             score(mt, 0, staged, True)
-        nc.sync.dma_start(out=out_0[0:W, cols(0)].rearrange("(u p) c -> p u c", p=P), in_=staged[:, :, cols(0)])
         for mt in range(4):
             score(mt, 1, staged, True)
             if mt % 2 == 1:
-                nc.sync.dma_start(
-                    out=out_0[(mt - 1) * P : (mt + 1) * P, cols(1)].rearrange("(u p) c -> p u c", p=P),
-                    in_=staged[:, mt - 1 : mt + 1, cols(1)],
-                )
+                nc.sync.dma_start(out=paired_rows(out_0, mt // 2), in_=staged[:, mt - 1 : mt + 1, :])
         staged = tile("scores1", [P, 4, J], F32, "raw_w0")
         for mt in range(4, 6):
             for jh in range(2):
                 score(mt, jh, staged, True)
-            nc.sync.dma_start(out=out_0[mt * P : (mt + 1) * P, :], in_=staged[:, mt % 4, :])
+        nc.sync.dma_start(out=paired_rows(out_0, 2), in_=staged[:, 0:2, :])
 
         values = tile("values", [P, 4, J], F32)
         keys = [("v", 0, a) for a in range(2)]
         for nt in range(2):
             for jh in range(2):
                 against_table(keys, nt * P, jh, values[:, nt, :], 1.0, True)
-            nc.sync.dma_start(out=out_1[nt * P : (nt + 1) * P, :], in_=values[:, nt, :])
+        nc.sync.dma_start(out=paired_rows(out_1, 0), in_=values[:, 0:2, :])
 
         project(3, 0, on_both)
         project(3, 1, on_both)
@@ -295,8 +294,8 @@ def tile_list_mlat_scale_kernel(tc, x, w, tab_words, tab_scales, wv, offs, out_0
         for nt in range(2, 4):
             for jh in range(2):
                 against_table(keys, nt * P, jh, values[:, nt, :], 1.0, True)
-                nc.sync.dma_start(out=out_1[nt * P : (nt + 1) * P, cols(jh)], in_=values[:, nt, cols(jh)])
+                nc.sync.dma_start(out=paired_rows(out_1, 1)[:, nt % 2, cols(jh)], in_=values[:, nt, cols(jh)])
         for mt in range(6, 8):
             for jh in range(2):
                 score(mt, jh, staged, jh == 1)
-                nc.sync.dma_start(out=out_0[mt * P : (mt + 1) * P, cols(jh)], in_=staged[:, mt % 4, cols(jh)])
+                nc.sync.dma_start(out=paired_rows(out_0, 3)[:, mt % 2, cols(jh)], in_=staged[:, mt % 4, cols(jh)])

@@ -29,9 +29,12 @@ def tile_list_mlat_scale_kernel(tc, x, w, tab_words, tab_scales, wv, offs, out_0
     with ExitStack() as ctx:
         lists = ctx.enter_context(tc.tile_pool(name="lists", bufs=1))
         keep = ctx.enter_context(tc.tile_pool(name="keep", bufs=1))
+        chain = ctx.enter_context(tc.tile_pool(name="chain", bufs=1))
         psum = ctx.enter_context(tc.psum_pool(name="psum", bufs=8))
 
         def tile(name, shape, dtype, slot=None):
+            if isinstance(slot, int):
+                return chain.tile(shape, dtype, name=name, tag=name, align_bytes=64, offset=slot)
             return keep.tile(shape, dtype, name=name, tag=slot or name, align_bytes=64)
 
         def rows(a):
@@ -154,45 +157,44 @@ def tile_list_mlat_scale_kernel(tc, x, w, tab_words, tab_scales, wv, offs, out_0
                     stop=True,
                 )
 
-        def pick_words(jh, slot, parted_slot=None):
+        def pick_words(jh, slot):
             picked = tile("picked%d" % jh, [P, W], U32, slot)
             nc.vector.tensor_copy(picked[:], table[:].bitcast(U32).indirect(offsets[:, jh * W // 16 : (jh + 1) * W // 16]))
-            if jh == 0:
-                nc.tensor.matmul_mx(
-                    out=banks[1, 0, 0][:, 0:P],
-                    lhsT=codes["q", 0, 0][:, 0:P].bitcast(FP8X4),
-                    lhsT_scale=x_scales[1, 0][:, 0:P],
-                    rhs=picked[:, 0 : P // 2].bitcast(FP4X4),
-                    rhs_scale=x_scales[1, 0][:, P:HALF],
-                    start=True,
-                    stop=True,
+            return picked
+
+        def part_words(jh, picked):
+            parted[jh] = tile("parted%d" % jh, [P, 2, 2 * W], U8)
+            for d in range(2):
+                nc.vector.tensor_copy(
+                    out=parted[jh][:, d, :].bitcast(U16),
+                    in_=picked[:].bitcast(U16).rearrange("p (j d) -> p d j", d=2)[:, d, :],
                 )
-            parted[jh] = tile("parted%d" % jh, [P, 2, 2 * W], U8, parted_slot)
-            nc.vector.tensor_copy(
-                out=parted[jh][:].bitcast(U16),
-                in_=picked[:].bitcast(U16).rearrange("p (j d) -> p d j", d=2),
+
+        def table_pass(bank, keys, c0, jh, b):
+            nc.tensor.matmul_mx(
+                out=bank[:],
+                lhsT=codes[keys[b]][:, c0 : c0 + P].bitcast(FP8X4),
+                lhsT_scale=scales[keys[b]][:, c0 : c0 + P],
+                rhs=parted[jh][:, b, :].bitcast(FP4X4),
+                rhs_scale=tab_planes[:].bitcast(U8)[:, b * J + jh * W : b * J + (jh + 1) * W],
+                start=(b == 0),
+                stop=(b == 1),
             )
 
-        def against_table(keys, c0, jh, result, factor, on_scalar):
-            bank = psum.tile([P, W], F32, name="bank")
-            for b in range(2):
-                nc.tensor.matmul_mx(
-                    out=bank[:],
-                    lhsT=codes[keys[b]][:, c0 : c0 + P].bitcast(FP8X4),
-                    lhsT_scale=scales[keys[b]][:, c0 : c0 + P],
-                    rhs=parted[jh][:, b, :].bitcast(FP4X4),
-                    rhs_scale=tab_planes[:].bitcast(U8)[:, b * J + jh * W : b * J + (jh + 1) * W],
-                    start=(b == 0),
-                    stop=(b == 1),
-                )
+        def against_table(keys, c0, jh, result, factor, on_scalar, opened=None):
+            bank = opened
+            if opened is None:
+                bank = psum.tile([P, W], F32, name="bank")
+                table_pass(bank, keys, c0, jh, 0)
+            table_pass(bank, keys, c0, jh, 1)
             if on_scalar:
                 nc.scalar.activation(out=result[:, cols(jh)], in_=bank[:], func=COPY, scale=factor)
             else:
                 nc.vector.tensor_scalar_mul(out=result[:, cols(jh)], in0=bank[:], scalar1=factor)
 
-        def score(mt, jh, staged, on_scalar):
+        def score(mt, jh, staged, on_scalar, opened=None):
             keys = [("q", mt // 2, b) for b in range(2)]
-            against_table(keys, (mt % 2) * P, jh, staged[:, mt % 4, :], SCORE_SCALE, on_scalar)
+            against_table(keys, (mt % 2) * P, jh, staged[:, mt % 4, :], SCORE_SCALE, on_scalar, opened)
 
         offsets = lists.tile([P, J // 16], U16, name="offsets")
         scale_rows = tile("scale_rows", [P, T // 4], I32, "raw_v0")
@@ -219,7 +221,7 @@ def tile_list_mlat_scale_kernel(tc, x, w, tab_words, tab_scales, wv, offs, out_0
             quantise_x(0, pair, early_x[0], pair * HALF, early_casts[pair])
         nc.vector.tensor_copy(picked_scales[:], scale_rows[:].bitcast(U8).indirect(offsets[:]))
         for quad in range(4):
-            nc.sync.dma_start(
+            nc.gpsimd.dma_start(
                 out=tab_planes[32 * quad : 32 * quad + 4, :],
                 in_=picked_scales[32 * quad : 32 * quad + 32 : 4, :].bitcast(I32),
             )
@@ -244,17 +246,19 @@ def tile_list_mlat_scale_kernel(tc, x, w, tab_words, tab_scales, wv, offs, out_0
         quantise_x(1, 2, third_x1, 0, early_casts[2])
 
         project(0, 0, on_both)
-        project(0, 1, on_both, "first_chain")
+        project(0, 1, on_both, 0)
         quantise_qa(0)
         project(1, 0, on_scalar)
         project(1, 1, on_scalar)
         project(2, 0, on_scalar, "after_q20")
         project(2, 1, on_scalar, "after_q2")
+        keep_warm(banks[2, 0, 0], 1, 0)
         quantise_qa_half(1, 0)
-        pick_words(0, "first_chain")
-        quantise_qa_half(1, 1, "x_scales10")
-        pick_words(1, "first_chain")
-        quantise_qa_half(2, 0, "first_chain")
+        part_words(0, pick_words(0, 0))
+        picked = pick_words(1, 1024)
+        quantise_qa_half(1, 1, 0)
+        part_words(1, picked)
+        quantise_qa_half(2, 0, 2048)
         quantise_qa_half(2, 1, "after_q20")
 
         for a in range(2):
@@ -269,8 +273,13 @@ def tile_list_mlat_scale_kernel(tc, x, w, tab_words, tab_scales, wv, offs, out_0
             quantise_x(a, 3, late_x[a], 0, nc.vector.tensor_copy)
 
         staged = tile("scores0", [P, 4, J], F32, "raw_w1")
-        for mt in range(4):
+        for mt in range(2):
             score(mt, 0, staged, True)
+        opened = [psum.tile([P, W], F32, name="bank") for e in range(2)]
+        for e in range(2):
+            table_pass(opened[e], [("q", 1, 0)], e * P, 0, 0)
+        for e in range(2):
+            score(2 + e, 0, staged, True, opened[e])
         for mt in range(4):
             score(mt, 1, staged, True)
             if mt % 2 == 1:

@@ -92,7 +92,8 @@ def tile_list_mlat_scale_kernel(tc, x, w, tab_words, tab_scales, wv, offs, out_0
         def both(vector_slot=None, scalar_slot=None):
             return [(nc.vector.tensor_copy, vector_slot), (nc.scalar.copy, scalar_slot)]
 
-        def quantise_x(a, pair, raw, c0, copy, slot=None):
+        def quantise_x(a, pair, raw, c0, copy, slot=None, scales_slot=None):
+            x_scales[a, pair] = tile("x_scales%d%d" % (a, pair), [P, HALF], U8, scales_slot)
             grouped = tile("grouped_x%d%d" % (a, pair), [P, HALF * PACK], BF16, slot)
             copy(
                 out=grouped[:].rearrange("p (c i j) -> p c j i", i=4, j=PACK),
@@ -133,8 +134,8 @@ def tile_list_mlat_scale_kernel(tc, x, w, tab_words, tab_scales, wv, offs, out_0
             qa_tiles[pair, b] = qa_bf
 
         def quantise_qa_half(pair, b, slot=None):
-            codes["q", pair, b] = tile("codes_q%d%d" % (pair, b), [P, HALF], U32, slot)
-            scales["q", pair, b] = tile("scales_q%d%d" % (pair, b), [P, HALF], U8)
+            codes["q", pair, b] = tile("codes_q%d%d" % (pair, b), [P, HALF], U32)
+            scales["q", pair, b] = tile("scales_q%d%d" % (pair, b), [P, HALF], U8, slot)
             nc.vector.quantize_mx(
                 out=codes["q", pair, b][:].bitcast(FP8X4), scales=scales["q", pair, b][:], in_=qa_tiles[pair, b][:]
             )
@@ -201,14 +202,14 @@ def tile_list_mlat_scale_kernel(tc, x, w, tab_words, tab_scales, wv, offs, out_0
         picked_scales = tile("picked_scales", [P, J], U8)
         tab_planes = tile("tab_planes", [P, 2 * J // 4], I32)
         x_codes = [tile("x_codes%d" % a, [P, M], U32) for a in range(2)]
-        x_scales = {(a, pair): tile("x_scales%d%d" % (a, pair), [P, HALF], U8) for pair in range(4) for a in range(2)}
+        x_scales = {}
         on_scalar = [nc.scalar.copy, nc.scalar.copy]
         on_both = [nc.scalar.copy, nc.vector.tensor_copy]
-        early_casts = [nc.vector.tensor_copy, nc.scalar.copy, nc.vector.tensor_copy]
+        early_casts = [nc.vector.tensor_copy, nc.scalar.copy, nc.vector.tensor_copy, nc.scalar.copy]
 
         nc.vector.memset(scale_rows[:], 0)
         nc.vector.memset(tab_planes[:], 0)
-        early_x = [load("early_x0", x[rows(0), 0:EARLY])]
+        first_x0 = load("first_x0", x[rows(0), 0:EARLY])
         nc.sync.dma_start(offsets[:], offs)
         nc.sync.dma_start(out=scale_rows[0:P:4, :], in_=tab_scales.bitcast(I32).rearrange("a q n -> q a n"))
         raw_w = [load("raw_w%d" % a, w[rows(a), :]) for a in range(2)]
@@ -217,20 +218,25 @@ def tile_list_mlat_scale_kernel(tc, x, w, tab_words, tab_scales, wv, offs, out_0
         table = tile("table", [P, T], I32)
         nc.sync.dma_start(out=table[:], in_=tab_words[0].rearrange("p t b -> p (t b)").bitcast(I32))
 
-        for pair in range(3):
-            quantise_x(0, pair, early_x[0], pair * HALF, early_casts[pair])
+        quantise_x(0, 2, first_x0, W, nc.vector.tensor_copy)
         nc.vector.tensor_copy(picked_scales[:], scale_rows[:].bitcast(U8).indirect(offsets[:]))
         for quad in range(4):
             nc.gpsimd.dma_start(
                 out=tab_planes[32 * quad : 32 * quad + 4, :],
                 in_=picked_scales[32 * quad : 32 * quad + 32 : 4, :].bitcast(I32),
             )
-        raw_v = [load("raw_v0", wv[rows(0), :])]
-        quantise(("w", 0, 0), raw_w[0][:, :, cols(0)], both("raw_v1", "late_x0"))
-        raw_v.append(load("raw_v1", wv[rows(1), :]))
+        raw_wv = tile("raw_v0", [P, 2, PACK, N], F32)
+        nc.sync.dma_start(
+            out=raw_wv[:].rearrange("p a j n -> p a (j n)"), in_=wv.rearrange("(a p j) n -> p a (j n)", a=2, j=PACK)
+        )
+        raw_v = [raw_wv[:, a] for a in range(2)]
+        quantise(("w", 0, 0), raw_w[0][:, :, cols(0)], both("late_x0", "after_w00"))
         late_x = [load("late_x0", x[rows(0), EARLY:M])]
-        quantise(("w", 1, 0), raw_w[0][:, :, cols(1)], both(None, "late_x1"))
+        quantise(("w", 1, 0), raw_w[0][:, :, cols(1)], both("after_w10", "late_x1"))
         late_x.append(load("late_x1", x[rows(1), EARLY:M]))
+
+        for pair in range(2):
+            quantise_x(0, pair, first_x0, pair * HALF, early_casts[pair], None, "after_w%d0" % (1 - pair))
 
         first_banks = [(pair, b, u) for pair in range(2) for b in range(2) for u in range(2)]
         for pair, b, u in first_banks[:-1]:
@@ -239,56 +245,68 @@ def tile_list_mlat_scale_kernel(tc, x, w, tab_words, tab_scales, wv, offs, out_0
         for b in range(2):
             quantise(("w", b, 1), raw_w[1][:, :, cols(b)], both())
             keep_warm(warm, b, 0)
-        keep_warm(warm, 1, HALF)
         project_passes(1, 1, 1, [(t, 0) for t in range(PACK)])
         for pair in range(2):
             quantise_x(1, pair, first_x1, pair * HALF, early_casts[pair])
-        quantise_x(1, 2, third_x1, 0, early_casts[2])
+        quantise_x(1, 2, third_x1, 0, nc.vector.tensor_copy)
 
         project(0, 0, on_both)
-        project(0, 1, on_both, 0)
+        project(0, 1, on_both)
         quantise_qa(0)
         project(1, 0, on_scalar)
         project(1, 1, on_scalar)
-        project(2, 0, on_scalar, "after_q20")
-        project(2, 1, on_scalar, "after_q2")
-        keep_warm(banks[2, 0, 0], 1, 0)
         quantise_qa_half(1, 0)
-        part_words(0, pick_words(0, 0))
-        picked = pick_words(1, 1024)
+        project(2, 0, on_scalar)
+        project(2, 1, on_scalar)
+        keep_warm(banks[1, 1, 1], 1, 0)
+        picked = pick_words(0, 0)
+        for repeat in range(2):
+            nc.tensor.matmul_mx(
+                out=banks[1, 1, 1][:],
+                lhsT=codes["q", 0, 0][:, 0:P].bitcast(FP8X4),
+                lhsT_scale=scales["q", 0, 0][:, 0:P],
+                rhs=picked[:].bitcast(U8)[:, 0 : 2 * W].bitcast(FP4X4),
+                rhs_scale=tab_planes[:].bitcast(U8)[:, 0:W],
+                start=True,
+                stop=True,
+            )
+        part_words(0, picked)
         quantise_qa_half(1, 1, 0)
+        quantise_qa_half(2, 0, 256)
+        picked = pick_words(1, 1024)
+        quantise_qa_half(2, 1, 512)
         part_words(1, picked)
-        quantise_qa_half(2, 0, 2048)
-        quantise_qa_half(2, 1, "after_q20")
 
         for a in range(2):
             operand(("v", 0, a))
         for s in range(2):
-            grouped_v = tile("grouped_v%d" % s, [P, 2, 2 * W], BF16, None if s else "after_q2")
+            grouped_v = tile("grouped_v%d" % s, [P, 2, 2 * W], BF16, "late_x1" if s else 2048)
             for a in range(2):
                 cast_half(nc.vector.tensor_copy, grouped_v[:, a, :], raw_v[a], s)
             for a in range(2):
                 quantise_half(("v", 0, a), s, grouped_v[:, a, :])
-        for a in range(2):
-            quantise_x(a, 3, late_x[a], 0, nc.vector.tensor_copy)
+            if s == 0:
+                for a in range(2):
+                    quantise_x(a, 3, late_x[a], 0, nc.vector.tensor_copy)
 
-        staged = tile("scores0", [P, 4, J], F32, "raw_w1")
-        for mt in range(2):
-            score(mt, 0, staged, True)
-        opened = [psum.tile([P, W], F32, name="bank") for e in range(2)]
-        for e in range(2):
-            table_pass(opened[e], [("q", 1, 0)], e * P, 0, 0)
-        for e in range(2):
-            score(2 + e, 0, staged, True, opened[e])
-        for mt in range(4):
-            score(mt, 1, staged, True)
-            if mt % 2 == 1:
-                nc.sync.dma_start(out=paired_rows(out_0, mt // 2), in_=staged[:, mt - 1 : mt + 1, :])
-        staged = tile("scores1", [P, 4, J], F32, "raw_w0")
-        for mt in range(4, 6):
-            for jh in range(2):
-                score(mt, jh, staged, True)
-        nc.sync.dma_start(out=paired_rows(out_0, 2), in_=staged[:, 0:2, :])
+        staged = [tile("scores0", [P, 4, J], F32, "raw_w1"), tile("scores1", [P, 4, J], F32, "raw_w0")]
+
+        def store_scores(pair, jh):
+            rows_of_pair = staged[pair // 2][:, 2 * (pair % 2) : 2 * (pair % 2) + 2, cols(jh)]
+            nc.sync.dma_start(out=paired_rows(out_0, pair)[:, :, cols(jh)], in_=rows_of_pair)
+
+        for jh in range(2):
+            for pair in range(3):
+                opened = [None, None]
+                if pair == 0 or (pair, jh) == (2, 0):
+                    opened = [psum.tile([P, W], F32, name="bank") for e in range(2)]
+                    for e in range(2):
+                        table_pass(opened[e], [("q", pair, 0)], e * P, jh, 0)
+                for e in range(2):
+                    score(2 * pair + e, jh, staged[pair // 2], True, opened[e])
+                if pair < 2:
+                    store_scores(pair, jh)
+        nc.sync.dma_start(out=paired_rows(out_0, 2), in_=staged[1][:, 0:2, :])
 
         values = tile("values", [P, 4, J], F32)
         keys = [("v", 0, a) for a in range(2)]
@@ -306,5 +324,5 @@ def tile_list_mlat_scale_kernel(tc, x, w, tab_words, tab_scales, wv, offs, out_0
                 nc.sync.dma_start(out=paired_rows(out_1, 1)[:, nt % 2, cols(jh)], in_=values[:, nt, cols(jh)])
         for mt in range(6, 8):
             for jh in range(2):
-                score(mt, jh, staged, jh == 1)
-                nc.sync.dma_start(out=paired_rows(out_0, 3)[:, mt % 2, cols(jh)], in_=staged[:, mt % 4, cols(jh)])
+                score(mt, jh, staged[1], jh == 1)
+                nc.sync.dma_start(out=paired_rows(out_0, 3)[:, mt % 2, cols(jh)], in_=staged[1][:, mt % 4, cols(jh)])

@@ -260,16 +260,15 @@ def tile_list_mlat_scale_kernel(tc, x, w, tab_words, tab_scales, wv, offs, out_0
         project(2, 1, on_scalar)
         keep_warm(banks[1, 1, 1], 1, 0)
         picked = pick_words(0, 0)
-        for repeat in range(2):
-            nc.tensor.matmul_mx(
-                out=banks[1, 1, 1][:],
-                lhsT=codes["q", 0, 0][:, 0:P].bitcast(FP8X4),
-                lhsT_scale=scales["q", 0, 0][:, 0:P],
-                rhs=picked[:].bitcast(U8)[:, 0 : 2 * W].bitcast(FP4X4),
-                rhs_scale=tab_planes[:].bitcast(U8)[:, 0:W],
-                start=True,
-                stop=True,
-            )
+        nc.tensor.matmul_mx(
+            out=banks[1, 1, 1][:],
+            lhsT=codes["q", 0, 0][:, 0:P].bitcast(FP8X4),
+            lhsT_scale=scales["q", 0, 0][:, 0:P],
+            rhs=picked[:].bitcast(U8)[:, 0 : 2 * W].bitcast(FP4X4),
+            rhs_scale=tab_planes[:].bitcast(U8)[:, 0:W],
+            start=True,
+            stop=True,
+        )
         part_words(0, picked)
         quantise_qa_half(1, 1, 0)
         quantise_qa_half(2, 0, 256)
@@ -287,7 +286,12 @@ def tile_list_mlat_scale_kernel(tc, x, w, tab_words, tab_scales, wv, offs, out_0
                 quantise_half(("v", 0, a), s, grouped_v[:, a, :])
             if s == 0:
                 for a in range(2):
-                    quantise_x(a, 3, late_x[a], 0, nc.vector.tensor_copy)
+                    x_scales[a, 3] = tile("x_scales%d3" % a, [P, HALF], U8)
+                    grouped = tile("grouped_x%d3" % a, [P, HALF * PACK], BF16)
+                    cast_half(nc.vector.tensor_copy, grouped[:], late_x[a], 0)
+                    nc.vector.quantize_mx(
+                        out=x_codes[a][:, EARLY:M].bitcast(FP8X4), scales=x_scales[a, 3][:], in_=grouped[:]
+                    )
 
         staged = [tile("scores0", [P, 4, J], F32, "raw_w1"), tile("scores1", [P, 4, J], F32, "raw_w0")]
 
@@ -315,12 +319,26 @@ def tile_list_mlat_scale_kernel(tc, x, w, tab_words, tab_scales, wv, offs, out_0
                 against_table(keys, nt * P, jh, values[:, nt, :], 1.0, True)
         nc.sync.dma_start(out=paired_rows(out_1, 0), in_=values[:, 0:2, :])
 
-        project(3, 0, on_both)
-        project(3, 1, on_both)
-        quantise_qa(3)
+        for b in range(2):
+            codes["q", 3, b] = tile("codes_q3%d" % b, [P, HALF], U32)
+            scales["q", 3, b] = tile("scales_q3%d" % b, [P, HALF], U8)
         for nt in range(2, 4):
+            e = nt % 2
+            for b in range(2):
+                project_passes(3, b, e, [(t, a) for t in range(PACK) for a in range(2)])
+                qa_tiles[3, b, e] = tile("qa_bf3%d%d" % (b, e), [P, W], BF16)
+                on_both[b](
+                    out=qa_tiles[3, b, e][:].rearrange("p (q t) -> p q t", t=PACK),
+                    in_=banks[3, b, e][:].rearrange("p (t q) -> p q t", t=PACK),
+                )
+            for b in range(2):
+                nc.vector.quantize_mx(
+                    out=codes["q", 3, b][:, e * P : (e + 1) * P].bitcast(FP8X4),
+                    scales=scales["q", 3, b][:, e * P : (e + 1) * P],
+                    in_=qa_tiles[3, b, e][:],
+                )
             for jh in range(2):
-                against_table(keys, nt * P, jh, values[:, nt, :], 1.0, True)
+                against_table(keys, nt * P, jh, values[:, nt, :], 1.0, jh == 1)
                 nc.sync.dma_start(out=paired_rows(out_1, 1)[:, nt % 2, cols(jh)], in_=values[:, nt, cols(jh)])
         for mt in range(6, 8):
             for jh in range(2):

@@ -34,8 +34,8 @@ def tile_list_mlat_scale_kernel(tc, x, w, tab_words, tab_scales, wv, offs, out_0
 
         def tile(name, shape, dtype, slot=None):
             if isinstance(slot, int):
-                return chain.tile(shape, dtype, name=name, tag=name, align_bytes=64, offset=slot)
-            return keep.tile(shape, dtype, name=name, tag=slot or name, align_bytes=64)
+                return chain.tile(shape, dtype, name=name, tag=name, align_bytes=256, offset=slot)
+            return keep.tile(shape, dtype, name=name, tag=slot or name, align_bytes=256)
 
         def rows(a):
             return slice(a * KP, (a + 1) * KP)

@@ -221,7 +221,7 @@ def tile_list_mlat_scale_kernel(tc, x, w, tab_words, tab_scales, wv, offs, out_0
         quantise_x(0, 2, first_x0, W, nc.vector.tensor_copy)
         nc.vector.tensor_copy(picked_scales[:], scale_rows[:].bitcast(U8).indirect(offsets[:]))
         for quad in range(4):
-            nc.gpsimd.dma_start(
+            nc.sync.dma_start(
                 out=tab_planes[32 * quad : 32 * quad + 4, :],
                 in_=picked_scales[32 * quad : 32 * quad + 32 : 4, :].bitcast(I32),
             )

@@ -21,6 +21,7 @@ KP = P * PACK
 W = 512
 HALF = W // 2
 EARLY = 3 * HALF
+BANK = 2048
 SCORE_SCALE = 0.03125
 
 
@@ -30,12 +31,19 @@ def tile_list_mlat_scale_kernel(tc, x, w, tab_words, tab_scales, wv, offs, out_0
         lists = ctx.enter_context(tc.tile_pool(name="lists", bufs=1))
         keep = ctx.enter_context(tc.tile_pool(name="keep", bufs=1))
         chain = ctx.enter_context(tc.tile_pool(name="chain", bufs=1))
-        psum = ctx.enter_context(tc.psum_pool(name="psum", bufs=8))
+        psum = ctx.enter_context(tc.psum_pool(name="psum", bufs=1))
 
         def tile(name, shape, dtype, slot=None):
             if isinstance(slot, int):
                 return chain.tile(shape, dtype, name=name, tag=name, align_bytes=256, offset=slot)
             return keep.tile(shape, dtype, name=name, tag=slot or name, align_bytes=256)
+
+        taken = []
+
+        def bank_at(index):
+            taken.append(index)
+            name = "bank%d" % len(taken)
+            return psum.tile([P, W], F32, name=name, tag=name, offset=index * BANK)
 
         def rows(a):
             return slice(a * KP, (a + 1) * KP)
@@ -51,10 +59,8 @@ def tile_list_mlat_scale_kernel(tc, x, w, tab_words, tab_scales, wv, offs, out_0
         codes = {}
         scales = {}
 
-        def quantise(key, src, shares, codes_slot=None):
+        def quantise(key, src, shares, between=None, scales_slot=None):
             name = "%s%d%d" % key
-            codes[key] = tile("codes_" + name, [P, W], U32, codes_slot)
-            scales[key] = tile("scales_" + name, [P, W], U8)
             width = W // len(shares)
 
             def cast(s):
@@ -66,10 +72,14 @@ def tile_list_mlat_scale_kernel(tc, x, w, tab_words, tab_scales, wv, offs, out_0
                 )
                 return dst
 
+            made = [cast(s) for s in range(len(shares))]
+            if between:
+                between()
+            codes[key] = tile("codes_" + name, [P, W], U32)
+            scales[key] = tile("scales_" + name, [P, W], U8, scales_slot)
             for s in range(len(shares)):
-                dst = cast(s)
                 part = slice(s * width, (s + 1) * width)
-                nc.vector.quantize_mx(out=codes[key][:, part].bitcast(FP8X4), scales=scales[key][:, part], in_=dst[:])
+                nc.vector.quantize_mx(out=codes[key][:, part].bitcast(FP8X4), scales=scales[key][:, part], in_=made[s][:])
 
         def operand(key):
             name = "%s%d%d" % key
@@ -102,12 +112,35 @@ def tile_list_mlat_scale_kernel(tc, x, w, tab_words, tab_scales, wv, offs, out_0
             part = slice(pair * HALF, (pair + 1) * HALF)
             nc.vector.quantize_mx(out=x_codes[a][:, part].bitcast(FP8X4), scales=x_scales[a, pair][:], in_=grouped[:])
 
+        def quantise_paired(a, pair, raw):
+            x_scales[a, pair] = tile("x_scales%d%d" % (a, pair), [P, HALF], U8)
+            grouped = tile("grouped_x%d%d" % (a, pair), [P, HALF * PACK], BF16)
+            cast_half(nc.vector.tensor_copy, grouped[:], raw, 0)
+            part = slice(pair * HALF, (pair + 1) * HALF)
+            nc.vector.quantize_mx(out=x_codes[a][:, part].bitcast(FP8X4), scales=x_scales[a, pair][:], in_=grouped[:])
+
+        def project_tile(pair, e, steps, copies):
+            for b in range(2):
+                project_passes(pair, b, e, steps)
+                qa_tiles[pair, b, e] = tile("qa_bf%d%d%d" % (pair, b, e), [P, W], BF16)
+                copies[b](
+                    out=qa_tiles[pair, b, e][:].rearrange("p (q t) -> p q t", t=PACK),
+                    in_=banks[pair, b, e][:].rearrange("p (t q) -> p q t", t=PACK),
+                )
+            for b in range(2):
+                if e == 0:
+                    codes["q", pair, b] = tile("codes_q%d%d" % (pair, b), [P, HALF], U32)
+                    scales["q", pair, b] = tile("scales_q%d%d" % (pair, b), [P, HALF], U8)
+                nc.vector.quantize_mx(
+                    out=codes["q", pair, b][:, e * P : (e + 1) * P].bitcast(FP8X4),
+                    scales=scales["q", pair, b][:, e * P : (e + 1) * P],
+                    in_=qa_tiles[pair, b, e][:],
+                )
+
         banks = {}
 
         def project_passes(pair, b, u, steps):
             m0 = pair * HALF + u * P
-            if (pair, b, u) not in banks:
-                banks[pair, b, u] = psum.tile([P, W], F32, name="bank")
             for t, a in steps:
                 nc.tensor.matmul_mx(
                     out=banks[pair, b, u][:, t * P : (t + 1) * P],
@@ -121,11 +154,10 @@ def tile_list_mlat_scale_kernel(tc, x, w, tab_words, tab_scales, wv, offs, out_0
 
         qa_tiles = {}
 
-        def project(pair, b, copies, slot=None):
+        def project(pair, b, copies, slot=None, both_passes=False):
             qa_bf = tile("qa_bf%d%d" % (pair, b), [P, 2 * W], BF16, slot)
             for u in range(2):
-                first = 1 if (pair, b, u) in banks else 0
-                project_passes(pair, b, u, [(t, a) for t in range(PACK) for a in range(first, 2)])
+                project_passes(pair, b, u, [(t, a) for t in range(PACK) for a in range(0 if both_passes else 1, 2)])
                 bank = banks[pair, b, u]
                 copies[u](
                     out=qa_bf[:].rearrange("p (e u q t) -> p u e q t", e=2, u=2, t=PACK)[:, u],
@@ -164,10 +196,10 @@ def tile_list_mlat_scale_kernel(tc, x, w, tab_words, tab_scales, wv, offs, out_0
             return picked
 
         def part_words(jh, picked):
-            parted[jh] = tile("parted%d" % jh, [P, 2, 2 * W], U8)
             for d in range(2):
+                parted[jh, d] = tile("parted%d%d" % (jh, d), [P, 2 * W], U8)
                 nc.vector.tensor_copy(
-                    out=parted[jh][:, d, :].bitcast(U16),
+                    out=parted[jh, d][:].bitcast(U16),
                     in_=picked[:].bitcast(U16).rearrange("p (j d) -> p d j", d=2)[:, d, :],
                 )
 
@@ -176,26 +208,24 @@ def tile_list_mlat_scale_kernel(tc, x, w, tab_words, tab_scales, wv, offs, out_0
                 out=bank[:],
                 lhsT=codes[keys[b]][:, c0 : c0 + P].bitcast(FP8X4),
                 lhsT_scale=scales[keys[b]][:, c0 : c0 + P],
-                rhs=parted[jh][:, b, :].bitcast(FP4X4),
+                rhs=parted[jh, b][:].bitcast(FP4X4),
                 rhs_scale=tab_planes[:].bitcast(U8)[:, b * J + jh * W : b * J + (jh + 1) * W],
                 start=(b == 0),
                 stop=(b == 1),
             )
 
-        def against_table(keys, c0, jh, result, factor, on_scalar, opened=None):
-            bank = opened
-            if opened is None:
-                bank = psum.tile([P, W], F32, name="bank")
-                table_pass(bank, keys, c0, jh, 0)
-            table_pass(bank, keys, c0, jh, 1)
-            if on_scalar:
-                nc.scalar.activation(out=result[:, cols(jh)], in_=bank[:], func=COPY, scale=factor)
-            else:
-                nc.vector.tensor_scalar_mul(out=result[:, cols(jh)], in0=bank[:], scalar1=factor)
-
-        def score(mt, jh, staged, on_scalar, opened=None):
-            keys = [("q", mt // 2, b) for b in range(2)]
-            against_table(keys, (mt % 2) * P, jh, staged[:, mt % 4, :], SCORE_SCALE, on_scalar, opened)
+        def against_table(keys, jobs, factor, open_first=False):
+            accs = [bank_at(index) for c0, jh, result, index, on_scalar in jobs]
+            if open_first:
+                for acc, (c0, jh, result, index, on_scalar) in zip(accs, jobs):
+                    table_pass(acc, keys, c0, jh, 0)
+            for acc, (c0, jh, result, index, on_scalar) in zip(accs, jobs):
+                for b in range(1 if open_first else 0, 2):
+                    table_pass(acc, keys, c0, jh, b)
+                if on_scalar:
+                    nc.scalar.activation(out=result[:, cols(jh)], in_=acc[:], func=COPY, scale=factor)
+                else:
+                    nc.vector.tensor_scalar_mul(out=result[:, cols(jh)], in0=acc[:], scalar1=factor)
 
         offsets = lists.tile([P, J // 16], U16, name="offsets")
         scale_rows = tile("scale_rows", [P, T // 4], I32, "raw_v0")
@@ -204,12 +234,13 @@ def tile_list_mlat_scale_kernel(tc, x, w, tab_words, tab_scales, wv, offs, out_0
         x_codes = [tile("x_codes%d" % a, [P, M], U32) for a in range(2)]
         x_scales = {}
         on_scalar = [nc.scalar.copy, nc.scalar.copy]
+        on_vector = [nc.vector.tensor_copy, nc.vector.tensor_copy]
         on_both = [nc.scalar.copy, nc.vector.tensor_copy]
         early_casts = [nc.vector.tensor_copy, nc.scalar.copy, nc.vector.tensor_copy, nc.scalar.copy]
 
         nc.vector.memset(scale_rows[:], 0)
         nc.vector.memset(tab_planes[:], 0)
-        first_x0 = load("first_x0", x[rows(0), 0:EARLY])
+        first_x0 = load("first_x0", x[rows(0), :])
         nc.sync.dma_start(offsets[:], offs)
         nc.sync.dma_start(out=scale_rows[0:P:4, :], in_=tab_scales.bitcast(I32).rearrange("a q n -> q a n"))
         raw_w = [load("raw_w%d" % a, w[rows(a), :]) for a in range(2)]
@@ -219,6 +250,7 @@ def tile_list_mlat_scale_kernel(tc, x, w, tab_words, tab_scales, wv, offs, out_0
         nc.sync.dma_start(out=table[:], in_=tab_words[0].rearrange("p t b -> p (t b)").bitcast(I32))
 
         quantise_x(0, 2, first_x0, W, nc.vector.tensor_copy)
+        quantise_paired(0, 3, first_x0[:, :, EARLY:M])
         nc.vector.tensor_copy(picked_scales[:], scale_rows[:].bitcast(U8).indirect(offsets[:]))
         for quad in range(4):
             nc.sync.dma_start(
@@ -230,24 +262,39 @@ def tile_list_mlat_scale_kernel(tc, x, w, tab_words, tab_scales, wv, offs, out_0
             out=raw_wv[:].rearrange("p a j n -> p a (j n)"), in_=wv.rearrange("(a p j) n -> p a (j n)", a=2, j=PACK)
         )
         raw_v = [raw_wv[:, a] for a in range(2)]
-        quantise(("w", 0, 0), raw_w[0][:, :, cols(0)], both("late_x0", "after_w00"))
-        late_x = [load("late_x0", x[rows(0), EARLY:M])]
+        quantise(("w", 0, 0), raw_w[0][:, :, cols(0)], both(None, "after_w00"))
         quantise(("w", 1, 0), raw_w[0][:, :, cols(1)], both("after_w10", "late_x1"))
-        late_x.append(load("late_x1", x[rows(1), EARLY:M]))
+        late_x1 = load("late_x1", x[rows(1), EARLY:M])
 
         for pair in range(2):
             quantise_x(0, pair, first_x0, pair * HALF, early_casts[pair], None, "after_w%d0" % (1 - pair))
 
         first_banks = [(pair, b, u) for pair in range(2) for b in range(2) for u in range(2)]
-        for pair, b, u in first_banks[:-1]:
+        for index, (pair, b, u) in enumerate(first_banks[:-1]):
+            banks[pair, b, u] = bank_at(index)
             project_passes(pair, b, u, [(t, 0) for t in range(PACK)])
-        warm = psum.tile([P, W], F32, name="bank")
-        for b in range(2):
-            quantise(("w", b, 1), raw_w[1][:, :, cols(b)], both())
-            keep_warm(warm, b, 0)
+        warm = bank_at(7)
+        quantise(("w", 0, 1), raw_w[1][:, :, cols(0)], both())
+        keep_warm(warm, 0, 0)
+        banks[1, 1, 1] = bank_at(7)
         project_passes(1, 1, 1, [(t, 0) for t in range(PACK)])
-        for pair in range(2):
-            quantise_x(1, pair, first_x1, pair * HALF, early_casts[pair])
+
+        def first_tokens():
+            x_scales[1, 0] = tile("x_scales10", [P, HALF], U8)
+            halves = [tile("grouped_x10%d" % u, [P, P * PACK], BF16, 8192 + 1024 * u) for u in range(2)]
+            for u in range(2):
+                nc.vector.tensor_copy(
+                    out=halves[u][:].rearrange("p (c i j) -> p c j i", i=4, j=PACK),
+                    in_=first_x1[:, :, u * P : (u + 1) * P].rearrange("p j (c i) -> p c j i", i=4),
+                )
+            for u in range(2):
+                part = slice(u * P, (u + 1) * P)
+                nc.vector.quantize_mx(
+                    out=x_codes[1][:, part].bitcast(FP8X4), scales=x_scales[1, 0][:, part], in_=halves[u][:]
+                )
+
+        quantise(("w", 1, 1), raw_w[1][:, :, cols(1)], both(), first_tokens, 8192)
+        quantise_x(1, 1, first_x1, HALF, nc.scalar.copy)
         quantise_x(1, 2, third_x1, 0, nc.vector.tensor_copy)
 
         project(0, 0, on_both)
@@ -255,13 +302,18 @@ def tile_list_mlat_scale_kernel(tc, x, w, tab_words, tab_scales, wv, offs, out_0
         quantise_qa(0)
         project(1, 0, on_scalar)
         project(1, 1, on_scalar)
-        quantise_qa_half(1, 0)
-        project(2, 0, on_scalar)
-        project(2, 1, on_scalar)
-        keep_warm(banks[1, 1, 1], 1, 0)
+        quantise_qa(1)
+        for b in range(2):
+            for u in range(2):
+                banks[2, b, u] = bank_at(2 * b + u)
+            project(2, b, on_scalar, both_passes=True)
+        for e in range(2):
+            for b in range(2):
+                banks[3, b, e] = bank_at(4 + 2 * e + b)
+                project_passes(3, b, e, [(t, 0) for t in range(PACK)])
         picked = pick_words(0, 0)
         nc.tensor.matmul_mx(
-            out=banks[1, 1, 1][:],
+            out=bank_at(0)[:],
             lhsT=codes["q", 0, 0][:, 0:P].bitcast(FP8X4),
             lhsT_scale=scales["q", 0, 0][:, 0:P],
             rhs=picked[:].bitcast(U8)[:, 0 : 2 * W].bitcast(FP4X4),
@@ -270,7 +322,6 @@ def tile_list_mlat_scale_kernel(tc, x, w, tab_words, tab_scales, wv, offs, out_0
             stop=True,
         )
         part_words(0, picked)
-        quantise_qa_half(1, 1, 0)
         quantise_qa_half(2, 0, 256)
         picked = pick_words(1, 1024)
         quantise_qa_half(2, 1, 512)
@@ -278,69 +329,38 @@ def tile_list_mlat_scale_kernel(tc, x, w, tab_words, tab_scales, wv, offs, out_0
 
         for a in range(2):
             operand(("v", 0, a))
-        for s in range(2):
-            grouped_v = tile("grouped_v%d" % s, [P, 2, 2 * W], BF16, "late_x1" if s else 2048)
+
+        def quantise_wv(s, slot):
+            grouped_v = tile("grouped_v%d" % s, [P, 2, 2 * W], BF16, slot)
             for a in range(2):
                 cast_half(nc.vector.tensor_copy, grouped_v[:, a, :], raw_v[a], s)
             for a in range(2):
                 quantise_half(("v", 0, a), s, grouped_v[:, a, :])
-            if s == 0:
-                for a in range(2):
-                    x_scales[a, 3] = tile("x_scales%d3" % a, [P, HALF], U8)
-                    grouped = tile("grouped_x%d3" % a, [P, HALF * PACK], BF16)
-                    cast_half(nc.vector.tensor_copy, grouped[:], late_x[a], 0)
-                    nc.vector.quantize_mx(
-                        out=x_codes[a][:, EARLY:M].bitcast(FP8X4), scales=x_scales[a, 3][:], in_=grouped[:]
-                    )
+
+        quantise_wv(0, 2048)
+        quantise_paired(1, 3, late_x1)
 
         staged = [tile("scores0", [P, 4, J], F32, "raw_w1"), tile("scores1", [P, 4, J], F32, "raw_w0")]
-
-        def store_scores(pair, jh):
-            rows_of_pair = staged[pair // 2][:, 2 * (pair % 2) : 2 * (pair % 2) + 2, cols(jh)]
-            nc.sync.dma_start(out=paired_rows(out_0, pair)[:, :, cols(jh)], in_=rows_of_pair)
-
         for jh in range(2):
             for pair in range(3):
-                opened = [None, None]
-                if pair == 0 or (pair, jh) == (2, 0):
-                    opened = [psum.tile([P, W], F32, name="bank") for e in range(2)]
-                    for e in range(2):
-                        table_pass(opened[e], [("q", pair, 0)], e * P, jh, 0)
-                for e in range(2):
-                    score(2 * pair + e, jh, staged[pair // 2], True, opened[e])
-                if pair < 2:
-                    store_scores(pair, jh)
-        nc.sync.dma_start(out=paired_rows(out_0, 2), in_=staged[1][:, 0:2, :])
+                tiles = staged[pair // 2][:, 2 * (pair % 2) : 2 * (pair % 2) + 2, :]
+                jobs = [(e * P, jh, tiles[:, e, :], 2 * ((jh + pair) % 2) + e, (jh, pair, e) != (1, 2, 1)) for e in range(2)]
+                against_table([("q", pair, b) for b in range(2)], jobs, SCORE_SCALE)
+                nc.sync.dma_start(out=paired_rows(out_0, pair)[:, :, cols(jh)], in_=tiles[:, :, cols(jh)])
 
+        quantise_wv(1, "late_x1")
         values = tile("values", [P, 4, J], F32)
         keys = [("v", 0, a) for a in range(2)]
         for nt in range(2):
+            against_table(keys, [(nt * P, jh, values[:, nt, :], 2 * nt + jh, True) for jh in range(2)], 1.0)
+            nc.sync.dma_start(out=paired_rows(out_1, 0)[:, nt, :], in_=values[:, nt, :])
+        for e in range(2):
+            project_tile(3, e, [(t, 1) for t in range(PACK)], on_both)
             for jh in range(2):
-                against_table(keys, nt * P, jh, values[:, nt, :], 1.0, True)
-        nc.sync.dma_start(out=paired_rows(out_1, 0), in_=values[:, 0:2, :])
-
-        for b in range(2):
-            codes["q", 3, b] = tile("codes_q3%d" % b, [P, HALF], U32)
-            scales["q", 3, b] = tile("scales_q3%d" % b, [P, HALF], U8)
-        for nt in range(2, 4):
-            e = nt % 2
-            for b in range(2):
-                project_passes(3, b, e, [(t, a) for t in range(PACK) for a in range(2)])
-                qa_tiles[3, b, e] = tile("qa_bf3%d%d" % (b, e), [P, W], BF16)
-                on_both[b](
-                    out=qa_tiles[3, b, e][:].rearrange("p (q t) -> p q t", t=PACK),
-                    in_=banks[3, b, e][:].rearrange("p (t q) -> p q t", t=PACK),
-                )
-            for b in range(2):
-                nc.vector.quantize_mx(
-                    out=codes["q", 3, b][:, e * P : (e + 1) * P].bitcast(FP8X4),
-                    scales=scales["q", 3, b][:, e * P : (e + 1) * P],
-                    in_=qa_tiles[3, b, e][:],
-                )
+                against_table(keys, [((2 + e) * P, jh, values[:, 2 + e, :], 2 * e + jh, jh == 1)], 1.0)
+                nc.sync.dma_start(out=paired_rows(out_1, 1)[:, e, cols(jh)], in_=values[:, 2 + e, cols(jh)])
+        keys = [("q", 3, b) for b in range(2)]
+        for e in range(2):
             for jh in range(2):
-                against_table(keys, nt * P, jh, values[:, nt, :], 1.0, jh == 1)
-                nc.sync.dma_start(out=paired_rows(out_1, 1)[:, nt % 2, cols(jh)], in_=values[:, nt, cols(jh)])
-        for mt in range(6, 8):
-            for jh in range(2):
-                score(mt, jh, staged[1], jh == 1)
-                nc.sync.dma_start(out=paired_rows(out_0, 3)[:, mt % 2, cols(jh)], in_=staged[1][:, mt % 4, cols(jh)])
+                against_table(keys, [(e * P, jh, staged[1][:, 2 + e, :], 4 + 2 * e + jh, jh == 1)], SCORE_SCALE)
+                nc.sync.dma_start(out=paired_rows(out_0, 3)[:, e, cols(jh)], in_=staged[1][:, 2 + e, cols(jh)])

@@ -112,10 +112,10 @@ def tile_list_mlat_scale_kernel(tc, x, w, tab_words, tab_scales, wv, offs, out_0
             part = slice(pair * HALF, (pair + 1) * HALF)
             nc.vector.quantize_mx(out=x_codes[a][:, part].bitcast(FP8X4), scales=x_scales[a, pair][:], in_=grouped[:])
 
-        def quantise_paired(a, pair, raw):
+        def quantise_paired(a, pair, raw, copy):
             x_scales[a, pair] = tile("x_scales%d%d" % (a, pair), [P, HALF], U8)
             grouped = tile("grouped_x%d%d" % (a, pair), [P, HALF * PACK], BF16)
-            cast_half(nc.vector.tensor_copy, grouped[:], raw, 0)
+            cast_half(copy, grouped[:], raw, 0)
             part = slice(pair * HALF, (pair + 1) * HALF)
             nc.vector.quantize_mx(out=x_codes[a][:, part].bitcast(FP8X4), scales=x_scales[a, pair][:], in_=grouped[:])
 
@@ -228,8 +228,8 @@ def tile_list_mlat_scale_kernel(tc, x, w, tab_words, tab_scales, wv, offs, out_0
                     nc.vector.tensor_scalar_mul(out=result[:, cols(jh)], in0=acc[:], scalar1=factor)
 
         offsets = lists.tile([P, J // 16], U16, name="offsets")
-        scale_rows = tile("scale_rows", [P, T // 4], I32, "raw_v0")
-        picked_scales = tile("picked_scales", [P, J], U8)
+        scale_rows = tile("scale_rows", [P, 2, T // 4], I32, "raw_v0")
+        picked_scales = tile("picked_scales", [P, 2, J], U8)
         tab_planes = tile("tab_planes", [P, 2 * J // 4], I32)
         x_codes = [tile("x_codes%d" % a, [P, M], U32) for a in range(2)]
         x_scales = {}
@@ -238,24 +238,29 @@ def tile_list_mlat_scale_kernel(tc, x, w, tab_words, tab_scales, wv, offs, out_0
         on_both = [nc.scalar.copy, nc.vector.tensor_copy]
         early_casts = [nc.vector.tensor_copy, nc.scalar.copy, nc.vector.tensor_copy, nc.scalar.copy]
 
-        nc.vector.memset(scale_rows[:], 0)
+        nc.vector.memset(scale_rows[:, 0, :], 0)
+        nc.gpsimd.memset(scale_rows[:, 1, :], 0)
         nc.vector.memset(tab_planes[:], 0)
-        first_x0 = load("first_x0", x[rows(0), :])
+        first_x0 = tile("first_x0", [P, PACK, M], F32)
+        x_rows = x[rows(0), :].rearrange("(p j) c -> p j c", j=PACK)
+        nc.sync.dma_start(out=first_x0[:, 0:2, :], in_=x_rows[:, 0:2, :])
         nc.sync.dma_start(offsets[:], offs)
-        nc.sync.dma_start(out=scale_rows[0:P:4, :], in_=tab_scales.bitcast(I32).rearrange("a q n -> q a n"))
+        nc.sync.dma_start(out=scale_rows[32:96:4], in_=tab_scales.bitcast(I32).rearrange("a q n -> q a n"))
+        nc.sync.dma_start(out=first_x0[:, 2:4, :], in_=x_rows[:, 2:4, :])
         raw_w = [load("raw_w%d" % a, w[rows(a), :]) for a in range(2)]
         first_x1 = load("first_x1", x[rows(1), 0:W])
         third_x1 = load("third_x1", x[rows(1), W:EARLY])
         table = tile("table", [P, T], I32)
         nc.sync.dma_start(out=table[:], in_=tab_words[0].rearrange("p t b -> p (t b)").bitcast(I32))
 
+        for a in range(2):
+            nc.vector.tensor_copy(picked_scales[:, a, :], scale_rows[:, a, :].bitcast(U8).indirect(offsets[:]))
         quantise_x(0, 2, first_x0, W, nc.vector.tensor_copy)
-        quantise_paired(0, 3, first_x0[:, :, EARLY:M])
-        nc.vector.tensor_copy(picked_scales[:], scale_rows[:].bitcast(U8).indirect(offsets[:]))
-        for quad in range(4):
+        quantise_paired(0, 3, first_x0[:, :, EARLY:M], nc.scalar.copy)
+        for r in range(4):
             nc.sync.dma_start(
-                out=tab_planes[32 * quad : 32 * quad + 4, :],
-                in_=picked_scales[32 * quad : 32 * quad + 32 : 4, :].bitcast(I32),
+                out=tab_planes[r:P:32, :],
+                in_=picked_scales[32 + 4 * r : 96 : 16].rearrange("p a j -> p (a j)").bitcast(I32),
             )
         raw_wv = tile("raw_v0", [P, 2, PACK, N], F32)
         nc.sync.dma_start(
@@ -338,7 +343,7 @@ def tile_list_mlat_scale_kernel(tc, x, w, tab_words, tab_scales, wv, offs, out_0
                 quantise_half(("v", 0, a), s, grouped_v[:, a, :])
 
         quantise_wv(0, 2048)
-        quantise_paired(1, 3, late_x1)
+        quantise_paired(1, 3, late_x1, nc.vector.tensor_copy)
 
         staged = [tile("scores0", [P, 4, J], F32, "raw_w1"), tile("scores1", [P, 4, J], F32, "raw_w0")]
         for jh in range(2):

@@ -22,6 +22,8 @@ W = 512
 HALF = W // 2
 EARLY = 3 * HALF
 BANK = 2048
+WORDS_SHIFT = 32
+SCALES_SHIFT = 64
 SCORE_SCALE = 0.03125
 
 
@@ -37,6 +39,9 @@ def tile_list_mlat_scale_kernel(tc, x, w, tab_words, tab_scales, wv, offs, out_0
             if isinstance(slot, int):
                 return chain.tile(shape, dtype, name=name, tag=name, align_bytes=256, offset=slot)
             return keep.tile(shape, dtype, name=name, tag=slot or name, align_bytes=256)
+
+        def shifted(name, width, dtype, shift, slot=None):
+            return tile(name, [P, shift + width], dtype, slot)[:, shift : shift + width]
 
         taken = []
 
@@ -75,16 +80,16 @@ def tile_list_mlat_scale_kernel(tc, x, w, tab_words, tab_scales, wv, offs, out_0
             made = [cast(s) for s in range(len(shares))]
             if between:
                 between()
-            codes[key] = tile("codes_" + name, [P, W], U32)
-            scales[key] = tile("scales_" + name, [P, W], U8, scales_slot)
+            codes[key] = shifted("codes_" + name, W, U32, WORDS_SHIFT)
+            scales[key] = shifted("scales_" + name, W, U8, SCALES_SHIFT, scales_slot)
             for s in range(len(shares)):
                 part = slice(s * width, (s + 1) * width)
                 nc.vector.quantize_mx(out=codes[key][:, part].bitcast(FP8X4), scales=scales[key][:, part], in_=made[s][:])
 
         def operand(key):
             name = "%s%d%d" % key
-            codes[key] = tile("codes_" + name, [P, W], U32)
-            scales[key] = tile("scales_" + name, [P, W], U8)
+            codes[key] = shifted("codes_" + name, W, U32, WORDS_SHIFT)
+            scales[key] = shifted("scales_" + name, W, U8, SCALES_SHIFT)
 
         def cast_half(copy, dst, raw, s):
             copy(
@@ -103,7 +108,7 @@ def tile_list_mlat_scale_kernel(tc, x, w, tab_words, tab_scales, wv, offs, out_0
             return [(nc.vector.tensor_copy, vector_slot), (nc.scalar.copy, scalar_slot)]
 
         def quantise_x(a, pair, raw, c0, copy, slot=None, scales_slot=None):
-            x_scales[a, pair] = tile("x_scales%d%d" % (a, pair), [P, HALF], U8, scales_slot)
+            x_scales[a, pair] = shifted("x_scales%d%d" % (a, pair), HALF, U8, SCALES_SHIFT, scales_slot)
             grouped = tile("grouped_x%d%d" % (a, pair), [P, HALF * PACK], BF16, slot)
             copy(
                 out=grouped[:].rearrange("p (c i j) -> p c j i", i=4, j=PACK),
@@ -113,7 +118,7 @@ def tile_list_mlat_scale_kernel(tc, x, w, tab_words, tab_scales, wv, offs, out_0
             nc.vector.quantize_mx(out=x_codes[a][:, part].bitcast(FP8X4), scales=x_scales[a, pair][:], in_=grouped[:])
 
         def quantise_paired(a, pair, raw, copy):
-            x_scales[a, pair] = tile("x_scales%d%d" % (a, pair), [P, HALF], U8)
+            x_scales[a, pair] = shifted("x_scales%d%d" % (a, pair), HALF, U8, SCALES_SHIFT)
             grouped = tile("grouped_x%d%d" % (a, pair), [P, HALF * PACK], BF16)
             cast_half(copy, grouped[:], raw, 0)
             part = slice(pair * HALF, (pair + 1) * HALF)
@@ -129,8 +134,8 @@ def tile_list_mlat_scale_kernel(tc, x, w, tab_words, tab_scales, wv, offs, out_0
                 )
             for b in range(2):
                 if e == 0:
-                    codes["q", pair, b] = tile("codes_q%d%d" % (pair, b), [P, HALF], U32)
-                    scales["q", pair, b] = tile("scales_q%d%d" % (pair, b), [P, HALF], U8)
+                    codes["q", pair, b] = shifted("codes_q%d%d" % (pair, b), HALF, U32, WORDS_SHIFT)
+                    scales["q", pair, b] = shifted("scales_q%d%d" % (pair, b), HALF, U8, SCALES_SHIFT)
                 nc.vector.quantize_mx(
                     out=codes["q", pair, b][:, e * P : (e + 1) * P].bitcast(FP8X4),
                     scales=scales["q", pair, b][:, e * P : (e + 1) * P],
@@ -166,8 +171,8 @@ def tile_list_mlat_scale_kernel(tc, x, w, tab_words, tab_scales, wv, offs, out_0
             qa_tiles[pair, b] = qa_bf
 
         def quantise_qa_half(pair, b, slot=None):
-            codes["q", pair, b] = tile("codes_q%d%d" % (pair, b), [P, HALF], U32)
-            scales["q", pair, b] = tile("scales_q%d%d" % (pair, b), [P, HALF], U8, slot)
+            codes["q", pair, b] = shifted("codes_q%d%d" % (pair, b), HALF, U32, WORDS_SHIFT)
+            scales["q", pair, b] = shifted("scales_q%d%d" % (pair, b), HALF, U8, SCALES_SHIFT, slot)
             nc.vector.quantize_mx(
                 out=codes["q", pair, b][:].bitcast(FP8X4), scales=scales["q", pair, b][:], in_=qa_tiles[pair, b][:]
             )
@@ -230,7 +235,7 @@ def tile_list_mlat_scale_kernel(tc, x, w, tab_words, tab_scales, wv, offs, out_0
         offsets = lists.tile([P, J // 16], U16, name="offsets")
         scale_rows = tile("scale_rows", [P, 2, T // 4], I32, "raw_v0")
         picked_scales = tile("picked_scales", [P, 2, J], U8)
-        tab_planes = tile("tab_planes", [P, 2 * J // 4], I32)
+        tab_planes = shifted("tab_planes", 2 * J // 4, I32, SCALES_SHIFT // 4)
         x_codes = [tile("x_codes%d" % a, [P, M], U32) for a in range(2)]
         x_scales = {}
         on_scalar = [nc.scalar.copy, nc.scalar.copy]
@@ -285,7 +290,7 @@ def tile_list_mlat_scale_kernel(tc, x, w, tab_words, tab_scales, wv, offs, out_0
         project_passes(1, 1, 1, [(t, 0) for t in range(PACK)])
 
         def first_tokens():
-            x_scales[1, 0] = tile("x_scales10", [P, HALF], U8)
+            x_scales[1, 0] = shifted("x_scales10", HALF, U8, SCALES_SHIFT)
             halves = [tile("grouped_x10%d" % u, [P, P * PACK], BF16, 8192 + 1024 * u) for u in range(2)]
             for u in range(2):
                 nc.vector.tensor_copy(
@@ -327,7 +332,7 @@ def tile_list_mlat_scale_kernel(tc, x, w, tab_words, tab_scales, wv, offs, out_0
             stop=True,
         )
         part_words(0, picked)
-        quantise_qa_half(2, 0, 256)
+        quantise_qa_half(2, 0, 0)
         picked = pick_words(1, 1024)
         quantise_qa_half(2, 1, 512)
         part_words(1, picked)

from contextlib import ExitStack

import concourse.mybir as mybir

K, R, M, T, N, J = 1024, 1024, 1024, 4096, 512, 1024
FLOPS = 2 * (K * R * M + R * M * J + R * N * J)

F32 = mybir.dt.float32
BF16 = mybir.dt.bfloat16
I32 = mybir.dt.int32
U32 = mybir.dt.uint32
U16 = mybir.dt.uint16
U8 = mybir.dt.uint8
FP8X4 = mybir.dt.float8_e4m3fn_x4
FP4X4 = mybir.dt.float4_e2m1fn_x4
COPY = mybir.ActivationFunctionType.Copy

P = 128
PACK = 4
KP = P * PACK
W = 512
HALF = W // 2
EARLY = 3 * HALF
BANK = 2048
WORDS_SHIFT = 32
SCALES_SHIFT = 64
SCORE_SCALE = 0.03125


def tile_list_mlat_scale_kernel(tc, x, w, tab_words, tab_scales, wv, offs, out_0, out_1):
    nc = tc.nc
    with ExitStack() as ctx:
        lists = ctx.enter_context(tc.tile_pool(name="lists", bufs=1))
        keep = ctx.enter_context(tc.tile_pool(name="keep", bufs=1))
        chain = ctx.enter_context(tc.tile_pool(name="chain", bufs=1))
        psum = ctx.enter_context(tc.psum_pool(name="psum", bufs=1))

        def tile(name, shape, dtype, slot=None):
            if isinstance(slot, int):
                return chain.tile(shape, dtype, name=name, tag=name, align_bytes=256, offset=slot)
            return keep.tile(shape, dtype, name=name, tag=slot or name, align_bytes=256)

        def shifted(name, width, dtype, shift, slot=None):
            return tile(name, [P, shift + width], dtype, slot)[:, shift : shift + width]

        taken = []

        def bank_at(index):
            taken.append(index)
            name = "bank%d" % len(taken)
            return psum.tile([P, W], F32, name=name, tag=name, offset=index * BANK)

        def rows(a):
            return slice(a * KP, (a + 1) * KP)

        def cols(h):
            return slice(h * W, (h + 1) * W)

        def load(name, src, slot=None):
            raw = tile(name, [P, PACK, src.shape[1]], F32, slot)
            nc.sync.dma_start(out=raw[:], in_=src.rearrange("(p j) c -> p j c", j=PACK))
            return raw

        codes = {}
        scales = {}

        def quantise(key, src, shares, between=None, scales_slot=None):
            name = "%s%d%d" % key
            width = W // len(shares)

            def cast(s):
                copy, slot = shares[s]
                dst = tile("grouped_%s_%d" % (name, s), [P, width * PACK], BF16, slot)
                copy(
                    out=dst[:].rearrange("p (t m j) -> p m j t", t=2, j=PACK),
                    in_=src.rearrange("p j (m t) -> p m j t", t=PACK)[:, :, :, 2 * s : 2 * s + 2],
                )
                return dst

            made = [cast(s) for s in range(len(shares))]
            if between:
                between()
            codes[key] = shifted("codes_" + name, W, U32, WORDS_SHIFT)
            scales[key] = shifted("scales_" + name, W, U8, SCALES_SHIFT, scales_slot)
            for s in range(len(shares)):
                part = slice(s * width, (s + 1) * width)
                nc.vector.quantize_mx(out=codes[key][:, part].bitcast(FP8X4), scales=scales[key][:, part], in_=made[s][:])

        def operand(key):
            name = "%s%d%d" % key
            codes[key] = shifted("codes_" + name, W, U32, WORDS_SHIFT)
            scales[key] = shifted("scales_" + name, W, U8, SCALES_SHIFT)

        def cast_half(copy, dst, raw, s):
            copy(
                out=dst.rearrange("p (e c i j) -> p c j i e", e=2, i=2, j=PACK),
                in_=raw[:, :, s * HALF : (s + 1) * HALF].rearrange("p j (c i e) -> p c j i e", i=2, e=2),
            )

        def paired_rows(out, pair):
            return out[pair * HALF : (pair + 1) * HALF, :].rearrange("(p e) c -> p e c", e=2)

        def quantise_half(key, s, src):
            part = slice(s * HALF, (s + 1) * HALF)
            nc.vector.quantize_mx(out=codes[key][:, part].bitcast(FP8X4), scales=scales[key][:, part], in_=src)

        def both(vector_slot=None, scalar_slot=None):
            return [(nc.vector.tensor_copy, vector_slot), (nc.scalar.copy, scalar_slot)]

        def quantise_x(a, pair, raw, c0, copy, slot=None, scales_slot=None):
            x_scales[a, pair] = shifted("x_scales%d%d" % (a, pair), HALF, U8, SCALES_SHIFT, scales_slot)
            grouped = tile("grouped_x%d%d" % (a, pair), [P, HALF * PACK], BF16, slot)
            copy(
                out=grouped[:].rearrange("p (c i j) -> p c j i", i=4, j=PACK),
                in_=raw[:, :, c0 : c0 + HALF].rearrange("p j (c i) -> p c j i", i=4),
            )
            part = slice(pair * HALF, (pair + 1) * HALF)
            nc.vector.quantize_mx(out=x_codes[a][:, part].bitcast(FP8X4), scales=x_scales[a, pair][:], in_=grouped[:])

        def quantise_paired(a, pair, raw, copy):
            x_scales[a, pair] = shifted("x_scales%d%d" % (a, pair), HALF, U8, SCALES_SHIFT)
            grouped = tile("grouped_x%d%d" % (a, pair), [P, HALF * PACK], BF16)
            cast_half(copy, grouped[:], raw, 0)
            part = slice(pair * HALF, (pair + 1) * HALF)
            nc.vector.quantize_mx(out=x_codes[a][:, part].bitcast(FP8X4), scales=x_scales[a, pair][:], in_=grouped[:])

        def project_tile(pair, e, steps, copies):
            for b in range(2):
                project_passes(pair, b, e, steps)
                qa_tiles[pair, b, e] = tile("qa_bf%d%d%d" % (pair, b, e), [P, W], BF16)
                copies[b](
                    out=qa_tiles[pair, b, e][:].rearrange("p (q t) -> p q t", t=PACK),
                    in_=banks[pair, b, e][:].rearrange("p (t q) -> p q t", t=PACK),
                )
            for b in range(2):
                if e == 0:
                    codes["q", pair, b] = shifted("codes_q%d%d" % (pair, b), HALF, U32, WORDS_SHIFT)
                    scales["q", pair, b] = shifted("scales_q%d%d" % (pair, b), HALF, U8, SCALES_SHIFT)
                nc.vector.quantize_mx(
                    out=codes["q", pair, b][:, e * P : (e + 1) * P].bitcast(FP8X4),
                    scales=scales["q", pair, b][:, e * P : (e + 1) * P],
                    in_=qa_tiles[pair, b, e][:],
                )

        banks = {}

        def project_passes(pair, b, u, steps):
            m0 = pair * HALF + u * P
            for t, a in steps:
                nc.tensor.matmul_mx(
                    out=banks[pair, b, u][:, t * P : (t + 1) * P],
                    lhsT=codes["w", b, a][:, t * P : (t + 1) * P].bitcast(FP8X4),
                    lhsT_scale=scales["w", b, a][:, t * P : (t + 1) * P],
                    rhs=x_codes[a][:, m0 : m0 + P].bitcast(FP8X4),
                    rhs_scale=x_scales[a, pair][:, u * P : (u + 1) * P],
                    start=(a == 0 and t == 0),
                    stop=(a == 1 and t == PACK - 1),
                )

        qa_tiles = {}

        def project(pair, b, copies, slot=None, both_passes=False):
            qa_bf = tile("qa_bf%d%d" % (pair, b), [P, 2 * W], BF16, slot)
            for u in range(2):
                project_passes(pair, b, u, [(t, a) for t in range(PACK) for a in range(0 if both_passes else 1, 2)])
                bank = banks[pair, b, u]
                copies[u](
                    out=qa_bf[:].rearrange("p (e u q t) -> p u e q t", e=2, u=2, t=PACK)[:, u],
                    in_=bank[:].rearrange("p (t q e) -> p e q t", t=PACK, e=2),
                )
            qa_tiles[pair, b] = qa_bf

        def quantise_qa_half(pair, b, slot=None):
            codes["q", pair, b] = shifted("codes_q%d%d" % (pair, b), HALF, U32, WORDS_SHIFT)
            scales["q", pair, b] = shifted("scales_q%d%d" % (pair, b), HALF, U8, SCALES_SHIFT, slot)
            nc.vector.quantize_mx(
                out=codes["q", pair, b][:].bitcast(FP8X4), scales=scales["q", pair, b][:], in_=qa_tiles[pair, b][:]
            )

        def quantise_qa(pair):
            for b in range(2):
                quantise_qa_half(pair, b)

        parted = {}

        def keep_warm(bank, b, c0):
            for repeat in range(2):
                nc.tensor.matmul_mx(
                    out=bank[:],
                    lhsT=codes["w", b, 1][:, c0 : c0 + P].bitcast(FP8X4),
                    lhsT_scale=scales["w", b, 1][:, c0 : c0 + P],
                    rhs=x_codes[0][:, 0:W].bitcast(FP8X4),
                    rhs_scale=scales["w", 0, 0][:],
                    start=True,
                    stop=True,
                )

        def pick_words(jh, slot):
            picked = tile("picked%d" % jh, [P, W], U32, slot)
            nc.vector.tensor_copy(picked[:], table[:].bitcast(U32).indirect(offsets[:, jh * W // 16 : (jh + 1) * W // 16]))
            return picked

        def part_words(jh, picked):
            for d in range(2):
                parted[jh, d] = tile("parted%d%d" % (jh, d), [P, 2 * W], U8)
                nc.vector.tensor_copy(
                    out=parted[jh, d][:].bitcast(U16),
                    in_=picked[:].bitcast(U16).rearrange("p (j d) -> p d j", d=2)[:, d, :],
                )

        def table_pass(bank, keys, c0, jh, b):
            nc.tensor.matmul_mx(
                out=bank[:],
                lhsT=codes[keys[b]][:, c0 : c0 + P].bitcast(FP8X4),
                lhsT_scale=scales[keys[b]][:, c0 : c0 + P],
                rhs=parted[jh, b][:].bitcast(FP4X4),
                rhs_scale=tab_planes[:].bitcast(U8)[:, b * J + jh * W : b * J + (jh + 1) * W],
                start=(b == 0),
                stop=(b == 1),
            )

        def against_table(keys, jobs, factor, open_first=False):
            accs = [bank_at(index) for c0, jh, result, index, on_scalar in jobs]
            if open_first:
                for acc, (c0, jh, result, index, on_scalar) in zip(accs, jobs):
                    table_pass(acc, keys, c0, jh, 0)
            for acc, (c0, jh, result, index, on_scalar) in zip(accs, jobs):
                for b in range(1 if open_first else 0, 2):
                    table_pass(acc, keys, c0, jh, b)
                if on_scalar:
                    nc.scalar.activation(out=result[:, cols(jh)], in_=acc[:], func=COPY, scale=factor)
                else:
                    nc.vector.tensor_scalar_mul(out=result[:, cols(jh)], in0=acc[:], scalar1=factor)

        offsets = lists.tile([P, J // 16], U16, name="offsets")
        scale_rows = tile("scale_rows", [P, 2, T // 4], I32, "raw_v0")
        picked_scales = tile("picked_scales", [P, 2, J], U8)
        tab_planes = shifted("tab_planes", 2 * J // 4, I32, SCALES_SHIFT // 4)
        x_codes = [tile("x_codes%d" % a, [P, M], U32) for a in range(2)]
        x_scales = {}
        on_scalar = [nc.scalar.copy, nc.scalar.copy]
        on_vector = [nc.vector.tensor_copy, nc.vector.tensor_copy]
        on_both = [nc.scalar.copy, nc.vector.tensor_copy]
        early_casts = [nc.vector.tensor_copy, nc.scalar.copy, nc.vector.tensor_copy, nc.scalar.copy]

        nc.vector.memset(scale_rows[:, 0, :], 0)
        nc.gpsimd.memset(scale_rows[:, 1, :], 0)
        nc.vector.memset(tab_planes[:], 0)
        first_x0 = tile("first_x0", [P, PACK, M], F32)
        x_rows = x[rows(0), :].rearrange("(p j) c -> p j c", j=PACK)
        nc.sync.dma_start(out=first_x0[:, 0:2, :], in_=x_rows[:, 0:2, :])
        nc.sync.dma_start(offsets[:], offs)
        nc.sync.dma_start(out=scale_rows[32:96:4], in_=tab_scales.bitcast(I32).rearrange("a q n -> q a n"))
        nc.sync.dma_start(out=first_x0[:, 2:4, :], in_=x_rows[:, 2:4, :])
        raw_w = [load("raw_w%d" % a, w[rows(a), :]) for a in range(2)]
        first_x1 = load("first_x1", x[rows(1), 0:W])
        third_x1 = load("third_x1", x[rows(1), W:EARLY])
        table = tile("table", [P, T], I32)
        nc.sync.dma_start(out=table[:], in_=tab_words[0].rearrange("p t b -> p (t b)").bitcast(I32))

        for a in range(2):
            nc.vector.tensor_copy(picked_scales[:, a, :], scale_rows[:, a, :].bitcast(U8).indirect(offsets[:]))
        quantise_x(0, 2, first_x0, W, nc.vector.tensor_copy)
        quantise_paired(0, 3, first_x0[:, :, EARLY:M], nc.scalar.copy)
        for r in range(4):
            nc.sync.dma_start(
                out=tab_planes[r:P:32, :],
                in_=picked_scales[32 + 4 * r : 96 : 16].rearrange("p a j -> p (a j)").bitcast(I32),
            )
        raw_wv = tile("raw_v0", [P, 2, PACK, N], F32)
        nc.sync.dma_start(
            out=raw_wv[:].rearrange("p a j n -> p a (j n)"), in_=wv.rearrange("(a p j) n -> p a (j n)", a=2, j=PACK)
        )
        raw_v = [raw_wv[:, a] for a in range(2)]
        quantise(("w", 0, 0), raw_w[0][:, :, cols(0)], both(None, "after_w00"))
        quantise(("w", 1, 0), raw_w[0][:, :, cols(1)], both("after_w10", "late_x1"))
        late_x1 = load("late_x1", x[rows(1), EARLY:M])

        for pair in range(2):
            quantise_x(0, pair, first_x0, pair * HALF, early_casts[pair], None, "after_w%d0" % (1 - pair))

        first_banks = [(pair, b, u) for pair in range(2) for b in range(2) for u in range(2)]
        for index, (pair, b, u) in enumerate(first_banks[:-1]):
            banks[pair, b, u] = bank_at(index)
            project_passes(pair, b, u, [(t, 0) for t in range(PACK)])
        warm = bank_at(7)
        quantise(("w", 0, 1), raw_w[1][:, :, cols(0)], both())
        keep_warm(warm, 0, 0)
        banks[1, 1, 1] = bank_at(7)
        project_passes(1, 1, 1, [(t, 0) for t in range(PACK)])

        def first_tokens():
            x_scales[1, 0] = shifted("x_scales10", HALF, U8, SCALES_SHIFT)
            halves = [tile("grouped_x10%d" % u, [P, P * PACK], BF16, 8192 + 1024 * u) for u in range(2)]
            for u in range(2):
                nc.vector.tensor_copy(
                    out=halves[u][:].rearrange("p (c i j) -> p c j i", i=4, j=PACK),
                    in_=first_x1[:, :, u * P : (u + 1) * P].rearrange("p j (c i) -> p c j i", i=4),
                )
            for u in range(2):
                part = slice(u * P, (u + 1) * P)
                nc.vector.quantize_mx(
                    out=x_codes[1][:, part].bitcast(FP8X4), scales=x_scales[1, 0][:, part], in_=halves[u][:]
                )

        quantise(("w", 1, 1), raw_w[1][:, :, cols(1)], both(), first_tokens, 8192)
        quantise_x(1, 1, first_x1, HALF, nc.scalar.copy)
        quantise_x(1, 2, third_x1, 0, nc.vector.tensor_copy)

        project(0, 0, on_both)
        project(0, 1, on_both)
        quantise_qa(0)
        project(1, 0, on_scalar)
        project(1, 1, on_scalar)
        quantise_qa(1)
        for b in range(2):
            for u in range(2):
                banks[2, b, u] = bank_at(2 * b + u)
            project(2, b, on_scalar, both_passes=True)
        for e in range(2):
            for b in range(2):
                banks[3, b, e] = bank_at(4 + 2 * e + b)
                project_passes(3, b, e, [(t, 0) for t in range(PACK)])
        picked = pick_words(0, 0)
        nc.tensor.matmul_mx(
            out=bank_at(0)[:],
            lhsT=codes["q", 0, 0][:, 0:P].bitcast(FP8X4),
            lhsT_scale=scales["q", 0, 0][:, 0:P],
            rhs=picked[:].bitcast(U8)[:, 0 : 2 * W].bitcast(FP4X4),
            rhs_scale=tab_planes[:].bitcast(U8)[:, 0:W],
            start=True,
            stop=True,
        )
        part_words(0, picked)
        quantise_qa_half(2, 0, 0)
        picked = pick_words(1, 1024)
        quantise_qa_half(2, 1, 512)
        part_words(1, picked)

        for a in range(2):
            operand(("v", 0, a))

        def quantise_wv(s, slot):
            grouped_v = tile("grouped_v%d" % s, [P, 2, 2 * W], BF16, slot)
            for a in range(2):
                cast_half(nc.vector.tensor_copy, grouped_v[:, a, :], raw_v[a], s)
            for a in range(2):
                quantise_half(("v", 0, a), s, grouped_v[:, a, :])

        quantise_wv(0, 2048)
        quantise_paired(1, 3, late_x1, nc.vector.tensor_copy)

        staged = [tile("scores0", [P, 4, J], F32, "raw_w1"), tile("scores1", [P, 4, J], F32, "raw_w0")]
        for jh in range(2):
            for pair in range(3):
                tiles = staged[pair // 2][:, 2 * (pair % 2) : 2 * (pair % 2) + 2, :]
                jobs = [(e * P, jh, tiles[:, e, :], 2 * ((jh + pair) % 2) + e, (jh, pair, e) != (1, 2, 1)) for e in range(2)]
                against_table([("q", pair, b) for b in range(2)], jobs, SCORE_SCALE)
                nc.sync.dma_start(out=paired_rows(out_0, pair)[:, :, cols(jh)], in_=tiles[:, :, cols(jh)])

        quantise_wv(1, "late_x1")
        values = tile("values", [P, 4, J], F32)
        keys = [("v", 0, a) for a in range(2)]
        for nt in range(2):
            against_table(keys, [(nt * P, jh, values[:, nt, :], 2 * nt + jh, True) for jh in range(2)], 1.0)
            nc.sync.dma_start(out=paired_rows(out_1, 0)[:, nt, :], in_=values[:, nt, :])
        for e in range(2):
            project_tile(3, e, [(t, 1) for t in range(PACK)], on_both)
            for jh in range(2):
                against_table(keys, [((2 + e) * P, jh, values[:, 2 + e, :], 2 * e + jh, jh == 1)], 1.0)
                nc.sync.dma_start(out=paired_rows(out_1, 1)[:, e, cols(jh)], in_=values[:, 2 + e, cols(jh)])
        keys = [("q", 3, b) for b in range(2)]
        for e in range(2):
            for jh in range(2):
                against_table(keys, [(e * P, jh, staged[1][:, 2 + e, :], 4 + 2 * e + jh, jh == 1)], SCORE_SCALE)
                nc.sync.dma_start(out=paired_rows(out_0, 3)[:, e, cols(jh)], in_=staged[1][:, 2 + e, cols(jh)])
